import numpy as np, ml_dtypes
CORES = [78,86,94,102,110,118]
N = 6
BF = ml_dtypes.bfloat16
W, U, SH, B, T, DEL, LIM = 3072, 1536, 1, 192, 7, 3, 18
def parts(rng):
    return (rng.integers(0, 64, (N, 8, 16, W)), rng.integers(0, W, (N, 8, 16, U)), rng.integers(0, W, (N, 8, 16, B)), rng.integers(0, W, (N, 8, B)), rng.integers(0, 64, (N, 8, 16, B)))
def pack(x, canal, trail, cut, z):
    return {"x": x.reshape(N, 128, W).astype(np.float32).astype(BF), "canal": np.ascontiguousarray(canal.reshape(N, 128, U)).astype(np.int32), "trail": np.ascontiguousarray(trail.reshape(N, 128, B)).astype(np.int32),
            "cut": np.ascontiguousarray(cut).astype(np.int32), "z": z.reshape(N, 128, B).astype(np.float32).astype(BF)}
def setup_inputs(rng):
    return pack(*parts(rng))
def setup_inputs_spread(rng):
    def low(*shape): return np.minimum((W * rng.random(shape) ** 3).astype(np.int64), W - 1)
    def size(n): return np.minimum((64.0 ** rng.random((N, 8, 1, n)) * rng.random((N, 8, 16, n))).astype(np.int64), 63)
    return pack(size(W), low(N, 8, 16, U), low(N, 8, 16, B), low(N, 8, B), size(B))
def tips(rng, *shape):
    q = rng.random(shape)
    return np.where(q < 0.36, 0, np.where(q < 0.72, W - 1, rng.integers(0, W, shape)))
def setup_inputs_ends(rng):
    k = rng.random((N, 8, 1, W)); x = np.where(k < 0.2, 0, np.where(k < 0.4, 63, 63 * rng.integers(0, 2, (N, 8, 16, W))))
    one = (np.arange(16).reshape(1, 1, 16, 1) == rng.integers(0, 16, (N, 8, 1, W))) & (rng.random((N, 8, 1, W)) < 0.15)
    x = np.where(one, np.where(x == 63, 62, 1), x)
    for q in (1, N - 1): x[q] = np.where(rng.random((8, 1, W)) < 0.3, 32 + LIM + rng.integers(0, 3, (8, 1, W)), x[q])
    k = rng.random((N, 8, 1, B)); z = np.where(k < 0.3, 0, np.where(k < 0.45, 63, 63 * rng.integers(0, 2, (N, 8, 16, B))))
    for q in (0, 1, N - 1): z[q] = np.repeat(63 * rng.integers(0, 2, (8, 1, B)), 16, axis=1)
    z[:, :, :, B - 1] = 0
    canal, trail, cut = tips(rng, N, 8, 16, U), tips(rng, N, 8, 16, B), tips(rng, N, 8, B); cut[:, :, B - 1] = W - 1
    for r in range(N):
        for g in range(8):
            a = 2 * int(rng.integers(W // 8, W // 4)); b = a - 1; rows = rng.permutation(15)[:2]
            x[r, g, :, 0] = 0 if r in (0, 1, N - 1) else 63 * ((r + g) % 2)
            x[r, g, :, W - 1] = 63; x[r, g, :, a] = 63; x[r, g, :, b] = 63; x[r, g, int(rng.integers(0, 16)), b] = 62
            canal[r, g, :, U - 1] = W - 1; canal[r, g, rows[0], U - 1] = a; canal[r, g, rows[1], U - 1] = b
    w = 16 - DEL
    for q in (1, N - 1): trail[q, :, w] = np.where(z[q, :, 0] == 0, W - 1, 0)
    trail[1, 0, w, 0] = W - 1 - trail[1, 0, w, 0]
    trail[0, :, w] = np.where(z[0, :, 0] == 0, 0, W - 1)
    for q in range(2, N - 1):
        trail[q, 7, w] = np.where((trail[q, 7, w] >> SH) == U - 1, 0, trail[q, 7, w]); trail[q, 7, w, B - 1] = W - 1
    return pack(x, canal, trail, cut, z)
def setup_inputs_corners(rng):
    x, canal, trail, cut, z = parts(rng); s = int(rng.integers(0, 8)); H = 1 << SH
    for r in range(N):
        for g in range(8):
            kind = (r + g + s) % 8
            if kind == 0: cut[r, g] = (0, W - 1, int(rng.integers(0, W)))[r % 3]
            if kind == 1:
                u = rng.integers(0, U, (16, 1)); u[16 - DEL] = U - 1; u[17 - DEL if DEL > 1 else 0] = 0
                trail[r, g] = (u << SH) + rng.integers(0, H, (16, B))
            if kind == 2: trail[r, g] = (np.argsort(rng.random((16, U)), axis=1)[:, :B] << SH) + rng.integers(0, H, (16, B))
            if kind == 3:
                canal[r, g] = (np.arange(U)[None, :] << SH) + rng.integers(0, H, (16, U))
                cut[r, g] = rng.permutation(W)[:B]; trail[r, g] = cut[r, g][None, :]
            if kind == 4: x[r, g] = 30 + rng.integers(0, 4, (16, W)); z[r, g] = 30 + rng.integers(0, 4, (16, B))
            if kind == 5: x[r, g] = rng.integers(0, 4, (16, W)); z[r, g] = rng.integers(60, 64, (16, B))
            if kind == 6:
                at = np.argsort(rng.random((16, W)), axis=0); n = rng.integers(8, 10, (1, W)); sg = 2 * rng.integers(0, 2, (16, W)) - 1
                x[r, g] = 24 + sg * np.where(at < n, LIM + 1, LIM); z[r, g] = 24
            if kind == 7:
                x[r, g] = rng.integers(60, 64, (16, 4))[:, rng.integers(0, 4, W)]
                canal[r, g] = -np.sort(-canal[r, g], axis=0); canal[r, g, :, ::5] = canal[r, g, :1, ::5]
    return pack(x, canal, trail, cut, z)
def setup_inputs_full(rng):
    x, canal, trail, cut, z = parts(rng); w = 16 - DEL; w1 = (17 - DEL) % 16; H = 1 << SH; q = B // 4
    for r in range(N):
        for g in range(8):
            v = rng.integers(0, 64, W); y = np.full(B, 16); l = canal[r, g]; h = trail[r, g]
            if r == 0:
                h[w] = (rng.permutation(U)[:B] << SH) + rng.integers(0, H, B); v[h[w]] = rng.integers(40, 59, B)
            elif r == 1:
                o = rng.permutation(W - H); best = o[:B]; low = o[B:]
                v = rng.integers(0, 21, W); v[best] = rng.integers(25, 33, B)
                u = rng.permutation(U)[:B]; cut[r, g] = (u << SH) + rng.integers(0, H, B)
                l[:] = low[rng.integers(0, len(low), (16, U))]; l[rng.integers(0, 16, B), u] = best
                h[:] = rng.integers(0, W - H, (16, B))
                h[w, :B - 1] = (rng.permutation(U - 1)[:B - 1] << SH) + rng.integers(0, H, B - 1); h[w, B - 1] = W - 1
            elif r == 2:
                a = np.flatnonzero((v >= 16) & (v <= 32)); h[w] = a[rng.integers(0, len(a), B)]; h[w1] = a[rng.integers(0, len(a), B)]
                if g in (0, 3, 7):
                    far = np.flatnonzero(v >= 40); i = 0 if g == 0 else B - 1 if g == 7 else int(rng.integers(0, B))
                    h[w, i] = far[int(rng.integers(0, len(far)))]
            else:
                v = rng.integers(0, 63, W); v[0] = 63; v[W - 1] = 63
                y = rng.integers(0, 64, B); i = rng.permutation(B); u = rng.permutation(U - 1)[:2 * q]
                y[i[:q]] = 63; y[i[q:2 * q]] = 0; cut[r, g, i[:2 * q]] = (u << SH) + rng.integers(0, H, 2 * q)
                l[:, u[:q]] = W - 1; l[:, u[q:]] = rng.integers(1, W - 1, (16, q))
                l[rng.integers(0, 2, q), u[q:]] = 0; l[rng.integers(13, 16, q), u[q:]] = W - 1
            x[r, g] = v; z[r, g] = y
            if r > 2: x[r, g, int(rng.integers(0, 16)), 0] = 62
    return pack(x, canal, trail, cut, z)
def setup_inputs_meet(rng):
    x, canal, trail, cut, z = parts(rng)
    for r in range(N):
        for g in range(8):
            s = rng.permutation(W)[:64]; s[0] = W - 1
            canal[r, g] = s[rng.integers(0, 64, (16, U))]; trail[r, g] = s[rng.integers(0, 64, (16, B))]; cut[r, g] = s[rng.integers(0, 64, B)]
    return pack(x, canal, trail, cut, z)
def check_inputs(d):
    bad = []
    for k, hi in (("x", 63), ("canal", W - 1), ("trail", W - 1), ("cut", W - 1), ("z", 63)):
        a = np.asarray(d[k]).astype(np.float64)
        if not (np.min(a) >= 0 and np.max(a) <= hi): bad.append("range of " + k)
        if not np.all(a == np.floor(a)): bad.append("whole numbers in " + k)
    return bad
def reference(x, canal, trail, cut, z):
    X = x.astype(np.float32).astype(np.int64).reshape(N, 8, 16, W); C = canal.astype(np.int64).reshape(N, 8, 16, U); G = trail.astype(np.int64).reshape(N, 8, 16, B)
    V = cut.astype(np.int64).reshape(N, 8, B); Z = z.astype(np.float32).astype(np.int64).reshape(N, 8, 16, B); skips = np.zeros(N, np.int64)
    for t in range(T):
        lim = LIM + (skips & 3); skips = np.zeros(N, np.int64); come = np.zeros_like(Z); row = (t + 16 - DEL) % 16
        for r in range(N):
            for g in range(8):
                a, l, h, q = X[r, g], C[r, g], G[r, g], Z[r, g]
                k = l[:, V[r, g] >> SH]
                score = np.add.reduce(np.maximum(a[:, k] - q[:, None, :], 0), axis=0)
                c = np.min(np.where(score == np.max(score, axis=0), k, W), axis=0)
                cut_off = np.sum(np.abs(a[:, h] - q[:, None, :]) > lim[r], axis=0) >= 9
                w = h[row] + 0; skip = cut_off[row]; xw = a[:, w]; xc = a[:, c]
                first = np.zeros(B, bool); first[np.unique(w >> SH, return_index=True)[1]] = True
                new = np.where(skip, np.minimum(xw + 4, 63), (xw + q) >> 1)
                a[:, w[first]] = new[:, first]
                m = first & ~skip; u = w[m] >> SH
                l[:, u] = np.where(cut_off[:, m], l[:, u], h[:, m])
                h[:] = np.where(cut_off, k, h); h[t] = c
                a[:, c] = xc >> 1
                V[r, g] = c; skips[r] += np.sum(skip)
                come[(r + 1 + t % (N - 1)) % N, g] = (q + xc) >> 1
        Z = come
    return {"yx": X.reshape(N, 128, W).astype(np.float32).astype(BF), "yl": C.reshape(N, 128, U).astype(np.float32), "yg": G.reshape(N, 128, B).astype(np.float32)}

@@ -1,0 +1,436 @@
+from concourse.mybir import dt, AluOpType, AxisListType, ActivationFunctionType
+
+W, U, B, T_STEPS = 3072, 1536, 192, 7
+NB = B // 16
+STARTS = [sum(B - 16 * m for m in range(i)) for i in range(NB + 1)]
+RUN = STARTS[NB]
+CMID = 1536
+XB = 192
+ROWS = [(t + 13) % 16 for t in range(T_STEPS)]
+
+f32, b16, f16, i32, u16 = "float32", "bfloat16", "float16", "int32", "uint16"
+_S = {
+    "X": ([128, W + B], b16), "CN": ([128, 3840], f32), "TR": ([128, B], f16), "TRu": ([128, B], u16),
+    "xraw": ([128, W], b16), "craw": ([128, U], i32), "traw": ([128, B], i32), "zraw": ([128, B], b16), "vraw": ([128, B], i32),
+    "Ku": ([128, B], u16), "Kf": ([128, B], f32), "Kp": ([128, 6, 32], f16), "V": ([128, 6, 32], f16),
+    "Xg1": ([128, W], b16), "Xg2": ([128, W], b16), "M1": ([128, NB, 256], b16),
+    "A2": ([128, 3, 1024], b16), "IND": ([128, 3, 1024], b16), "AR": ([128, B], b16), "IR": ([128, B], b16),
+    "Sc": ([128, B], f32), "ci": ([128, NB], i32), "cm": ([128, NB], i32), "ch": ([128, NB], i32), "cf": ([128, NB], f32),
+    "CL": ([128, NB], u16), "VH": ([128, NB], u16), "UL": ([128, NB], u16), "ULf": ([128, 16], f32), "Dg": ([128, B], f16),
+    "ACh": ([128, B], f16), "E": ([128, RUN], b16), "EC": ([128, RUN], b16), "sg": ([128, B], f32), "xcut": ([128, B], b16),
+    "WD": ([128, B], f32), "WS": ([128, B], f32), "wu": ([128, 24], i32), "LU": ([128, NB], u16), "wb": ([128, NB], f32),
+    "SQ": ([128, RUN], b16), "SW": ([128, RUN], b16), "NF": ([128, 32], f32), "e1": ([128, 24], f32), "WU": ([128, 24], f32),
+    "LH": ([128, NB], u16), "LCf": ([128, NB], f32), "LC": ([128, NB], u16), "skb": ([128, NB], b16), "skr": ([128, B], b16),
+    "H": ([128, B], b16), "Q": ([128, B], b16), "mQ": ([128, B], b16),
+    "D": ([128, B], f32), "sm": ([128, B], f32), "smt": ([128, B], f32), "tD": ([128, B], f32), "TRf": ([128, B], f32),
+    "Co": ([128, B], f32), "CG": ([128, B], f32), "cD": ([128, B], f32), "TF": ([128, B], f32),
+    "jnk": ([128, NB], f32), "Sa": ([128, 1], f32), "Si": ([128, 1], i32), "Sj": ([128, 1], i32), "LIM": ([128, 1], f32),
+    "qi": ([128, 1], i32), "qa": ([128, 1], i32), "qm": ([128, 1], f32), "rowm": ([128, 16], f32), "nrowm": ([128, 16], f32),
+    "thr": ([128, 16], f32), "half": ([128, 2], f32), "io1": ([128, 48], f32), "io2": ([128, 48], f32), "io3": ([128, 48], f32),
+    "REV": ([128, NB], u16), "RP": ([128, NB], u16), "ENDS": ([128, 2], u16), "DUM": ([128, 32], f32),
+    "J16": ([128, B], f32), "DM": ([128, B], f32), "RST": ([128, B], f32), "A0": ([128, B], f32), "MK": ([128, RUN], b16), "MB": ([128, RUN], b16),
+    "on": ([128, 144], f32), "on2": ([128, 144], f32), "BOf": ([128, 128], f32), "IDf": ([128, 128], f32), "sh0": ([128, 128], f32), "sh1": ([128, 128], f32),
+    "BOh": ([128, 128], f16), "BOb": ([128, 128], b16), "PD1": ([128, 144], b16), "PDN": ([128, 144], b16), "PDH": ([128, 144], f16),
+    "IDb": ([128, 128], b16), "NIb": ([128, 128], b16), "IDh": ([128, 128], f16), "IDm": ([128, T_STEPS * 128], f16), "RSL": ([128, T_STEPS * 128], f16),
+    "SWP": ([128, 512], f16), "zero": ([128, B], b16), "ONS": ([128, 128], b16), "vsh": ([128, B], i32), "vfh": ([128, B], f16), "vrf": ([128, B], f32),
+}
+for _t in range(T_STEPS):
+    _S["Z%d" % _t] = ([128, B], b16)
+    if _t < T_STEPS - 1:
+        _S["ZN%d" % _t] = ([128, B], b16)
+SCRATCH = {k: ("sbuf", s, d) for k, (s, d) in _S.items()}
+SCRATCH.update({
+    "PA": ("psum", [128, 1024], f32), "PB": ("psum", [128, 1024], f32),
+    "PZ": ("psum", [128, 512], f32), "PK": ("psum", [128, 512], f32), "PW": ("psum", [128, 512], f32), "PC": ("psum", [128, 512], f32),
+})
+SEMAPHORES = ["sv", "sp", "sa", "sg", "zsent"] + ["zs%d" % t for t in range(1, T_STEPS)] + ["d%d" % i for i in range(40)]
+
+
+def rank_program(g, core, T, topo):
+    rank = T.rank_of(core)
+    if rank is None:
+        return
+    O, AF = AluOpType, ActivationFunctionType
+    N = len(T.cores)
+    ENG = {"v": g.vector, "p": g.tensor, "a": g.scalar, "g": g, "s": g.sync}
+    cnt, known, wr, rd = {}, {}, {}, {}
+
+    def need(q, src, n):
+        if known.get((q, src), 0) < n:
+            known[(q, src)] = n
+            ENG[q].wait_ge(T.sem[src], n)
+
+    def deps(q, R, Wr, par):
+        own = "s" + q
+        for k in R:
+            if k in wr and not (q == "p" and wr[k][0] == own):
+                need(q, wr[k][0], wr[k][1])
+            if k[0] == "P":
+                for s, n in rd.get(k, {}).items():
+                    if s != own:
+                        need(q, s, n)
+        for k in Wr:
+            if k in wr and not (wr[k][0] == own and (par or q == "p")):
+                need(q, wr[k][0], wr[k][1])
+            for s, n in rd.get(k, {}).items():
+                if not (s == own and (par or q == "p")):
+                    need(q, s, n)
+
+    def note(src, n, R, Wr):
+        for k in R:
+            rd.setdefault(k, {})[src] = n
+        for k in Wr:
+            wr[k] = (src, n)
+            rd[k] = {}
+
+    def op(q, name, R, Wr, *a, par=False, **kw):
+        R, Wr = R.split(), Wr.split()
+        deps(q, R, Wr, par)
+        if q == "v":
+            e = g.vector
+            fn = {"tc": e.tensor_copy, "ts": e.tensor_scalar, "tt": e.tensor_tensor, "scan": e.tensor_tensor_scan,
+                  "ms": e.memset, "tr": e.transpose}[name]
+        elif q == "a":
+            fn = g.scalar.activation
+        elif q == "p":
+            fn = g.tensor.matmul
+        else:
+            fn = {"iota": g.iota, "sel": g.affine_select}[name]
+        src = "s" + q
+        cnt[src] = cnt.get(src, 0) + 1
+        fn(*a, **kw).then_inc(T.sem[src], 1)
+        note(src, cnt[src], R, Wr)
+
+    nd = [0]
+
+    def dma(q, R, Wr, out, in_):
+        R, Wr = R.split(), Wr.split()
+        deps(q, R, Wr, True)
+        s = "d%d" % nd[0]
+        nd[0] += 1
+        ENG[q].dma_start(out, in_).then_inc(T.sem[s], 16)
+        note(s, 16, R, Wr)
+        return s
+
+    def vtc(R, Wr, o, i, **k):
+        op("v", "tc", R, Wr, o, i, **k)
+
+    def vts(R, Wr, o, i, s1, o0, s2=None, o1=None, **k):
+        if o1 is None:
+            op("v", "ts", R, Wr, o, i, s1, None, o0, **k)
+        else:
+            op("v", "ts", R, Wr, o, i, s1, s2, o0, o1, **k)
+
+    def vtt(R, Wr, o, a, b, f, **k):
+        op("v", "tt", R, Wr, o, a, b, f, **k)
+
+    def act(R, Wr, o, i, f=AF.Copy, **k):
+        op("a", "act", R, Wr, o, i, f, **k)
+
+    def mm(R, Wr, o, l, r, st, sp):
+        op("p", "mm", R, Wr, o, l, r, st, sp)
+
+    dma("s", "", "craw0", T.craw[:, 0:768], T.canal[:, 0:768])
+    dma("a", "", "craw1", T.craw[:, 768:1536], T.canal[:, 768:1536])
+    op("v", "ms", "", "vraw", T.vraw[:], 0)
+    for j in range(8):
+        dma("sa"[j % 2], "vraw" if j < 2 else "", "vr%d" % j, T.vraw[16 * j:16 * j + 1, :], T.cut[j:j + 1, :])
+    VR = " ".join("vr%d" % j for j in range(8))
+    dma("s", "", "traw", T.traw[:], T.trail[:])
+    dma("a", "", "zraw", T.zraw[:], T.z[:])
+    for j in range(4):
+        dma("sa"[j % 2], "", "xraw%d" % j, T.xraw[:, 768 * j:768 * j + 768], T.x[:, 768 * j:768 * j + 768])
+    op("g", "iota", "", "qi", T.qi[:], [[1, 1]], 0, 1)
+    op("g", "iota", "", "J16", T.J16[:], [[0, 12], [1, 16]], 0, 0, allow_small_or_imprecise_dtypes=True)
+    op("g", "iota", "", "io1", T.io1[:], [[16, 48]], 0, 0, allow_small_or_imprecise_dtypes=True)
+    op("v", "ms", "", "on", T.on[:], 1.0)
+    op("v", "ms", "", "on2", T.on2[:], 0.0)
+    op("v", "ms", "on2", "on2", T.on2[:, 15::16], 1.0)
+    op("v", "ms", "", "fon", T.sh0[:], 1.0)
+    op("g", "sel", "on", "on", T.on[:, 0:128], T.on[:, 0:128], [[-16, 8], [0, 16]], O.is_ge, 0.0, 0, 1)
+    op("g", "sel", "on", "BOf", T.BOf[:], T.on[:, 0:128], [[16, 8], [0, 16]], O.is_ge, 0.0, 15, -1)
+    op("g", "sel", "on2", "on2", T.on2[:], T.on2[:], [[-16, 9], [0, 16]], O.is_ge, 0.0, 0, 1)
+    op("g", "sel", "on2", "on2", T.on2[:], T.on2[:], [[16, 9], [0, 16]], O.is_ge, 0.0, 15, -1)
+    op("g", "sel", "fon", "sh1", T.sh1[:], T.sh0[:], [[-1, 128]], O.is_equal, 0.0, -16, 1)
+    op("g", "sel", "fon sh1", "sh0", T.sh0[:], T.sh0[:], [[-1, 128]], O.is_equal, 0.0, 16, 1)
+    vts("qi", "qa", T.qa[:], T.qi[:], 15, O.bitwise_and)
+    vtc("qa", "qm", T.qm[:], T.qa[:])
+    vts("J16 qm", "DM", T.DM[:], T.J16[:], T.qm[:], O.is_equal)
+    vts("io1 qm", "io2", T.io2[:, 0:12], T.io1[:, 0:12], T.qm[:], O.add)
+    vts("io2", "REV", T.REV[:], T.io2[:, 0:12], -1.0, O.mult, 191.0, O.add)
+    vts("J16", "A0", T.A0[:], T.J16[:], 0.0, O.not_equal)
+    vtc("BOf", "BOh", T.BOh[:], T.BOf[:])
+    vts("J16 qm", "rowm", T.rowm[:], T.J16[:, 0:16], T.qm[:], O.is_equal)
+    vts("J16 qm", "nrowm", T.nrowm[:], T.J16[:, 0:16], T.qm[:], O.not_equal)
+    vts("rowm", "thr", T.thr[:], T.rowm[:], 1000.0, O.mult, 8.5, O.add)
+    vts("io1", "RP", T.RP[:], T.io1[:, 0:12], 0.0625, O.mult)
+    vts("J16 qm", "IDf0", T.IDf[:], T.J16[:, 0:128], T.qm[:], O.is_equal)
+    vtt("IDf0 BOf", "IDf", T.IDf[:], T.IDf[:], T.BOf[:], O.mult)
+    act("IDf", "IDb", T.IDb[:], T.IDf[:])
+    act("IDf", "NIb", T.NIb[:], T.IDf[:], AF.Copy, scale=-1.0)
+    act("on2", "PDN", T.PDN[:], T.on2[:], AF.Copy, scale=-4096.0)
+    act("BOf", "BOb", T.BOb[:], T.BOf[:])
+    act("zraw REV", "Z0", T.Z0[:], T.zraw[:].indirect(T.REV[:]), AF.Copy, bias=float(XB))
+    vts("vraw " + VR, "vsh", T.vsh[:], T.vraw[:], 1, O.arith_shift_right)
+    vtc("vsh", "vfh", T.vfh[:], T.vsh[:])
+    mm("BOh vfh", "PW", T.PW[:, 0:192], T.BOh[:], T.vfh[:], True, True)
+    act("PW", "vrf", T.vrf[:], T.PW[:, 0:192])
+    vtc("craw0", "CN", T.CN[:, 0:768], T.craw[:, 0:768])
+    vtt("vrf REV DM", "WD", T.WD[:], T.vrf[:].indirect(T.REV[:]), T.DM[:], O.mult)
+    op("v", "scan", "A0 WD", "WS", T.WS[:], T.A0[:], T.WD[:], 0.0, O.mult, O.add)
+    vtc("WS", "VH", T.VH[:], T.WS[:, 15::16])
+    vtc("craw1", "CN", T.CN[:, 768:1536], T.craw[:, 768:1536], par=True)
+    for j in range(3):
+        act("xraw%d" % j, "X", T.X[:, 768 * j:768 * j + 768], T.xraw[:, 768 * j:768 * j + 768], AF.Copy, bias=float(XB), par=True)
+    vts("xraw3", "X2", T.X[:, 2304:3072], T.xraw[:, 2304:3072], float(XB), O.add)
+    act("on2", "PD1", T.PD1[:], T.on2[:])
+    SWPS = "SWP00 SWP01 SWP10 SWP11"
+
+    def consts_a():
+        vts("traw REV", "TR", T.TR[:], T.traw[:].indirect(T.REV[:]), -float(CMID), O.add)
+        vts("TR", "TRu", T.TRu[:], T.TR[:], float(CMID), O.add)
+        vtc("IDf", "IDh", T.IDh[:], T.IDf[:])
+        vts("BOf rowm", "RSL0", T.RSL[:, 0:128], T.BOf[:], T.rowm[:, ROWS[0]:ROWS[0] + 1], O.mult)
+        op("v", "ms", "", "zero", T.zero[:], 0.0)
+
+    def consts_b():
+        vts("qi", "Si", T.Si[:], T.qi[:], 16, O.bitwise_and)
+        vts("Si", "half", T.half[:, 1:2], T.Si[:], 0.0625, O.mult)
+        vts("half", "half0", T.half[:, 0:1], T.half[:, 1:2], -1.0, O.mult, 1.0, O.add)
+        vts("IDf half half0", "SWP00", T.SWP[:, 0:128], T.IDf[:], T.half[:, 0:1], O.mult)
+        vts("sh0 half half0", "SWP10", T.SWP[:, 256:384], T.sh0[:], T.half[:, 0:1], O.mult)
+        vts("sh1 half half0", "SWP01", T.SWP[:, 128:256], T.sh1[:], T.half[:, 1:2], O.mult)
+        vts("IDf half half0", "SWP11", T.SWP[:, 384:512], T.IDf[:], T.half[:, 1:2], O.mult)
+
+    def consts_c():
+        vts("J16", "RST0", T.RST[:], T.J16[:], 0.0, O.is_equal, 2.0e8, O.mult)
+        vts("RST0", "RST", T.RST[:], T.RST[:], -1.0e8, O.add)
+        op("v", "ms", "", "DUM", T.DUM[:], 0.0)
+        vts("io2", "DUM", T.DUM[:, 0:12], T.io2[:, 0:12], float(W), O.add)
+        vts("io2", "DUM", T.DUM[:, 12:24], T.io2[:, 0:12], float(U), O.add)
+        vtc("io2", "io3", T.io3[:, 0:2], T.io2[:, 0:2])
+        for lim in (12.0, 24.0):
+            vts("io2", "io1b", T.io1[:, 16:18], T.io2[:, 0:2], lim, O.is_ge, -12.0, O.mult)
+            vtt("io3 io1b", "io3", T.io3[:, 0:2], T.io3[:, 0:2], T.io1[:, 16:18], O.add)
+        vts("io3", "io1b", T.io1[:, 16:18], T.io3[:, 0:2], -8.0, O.mult, 192.0, O.add)
+        vts("io3", "io1c", T.io1[:, 32:34], T.io3[:, 0:2], 1.0, O.add)
+        vtt("io1b io1c", "io3", T.io3[:, 4:6], T.io1[:, 16:18], T.io1[:, 32:34], O.mult)
+        vts("io3", "ENDS", T.ENDS[:], T.io3[:, 4:6], -1.0, O.add)
+        vtc("on2", "PDH", T.PDH[:], T.on2[:])
+        op("v", "ms", "", "LIM", T.LIM[:], 18.5)
+
+    def consts_d():
+        op("v", "ms", "", "onb", T.ONS[:], 1.0 / 2048.0)
+        op("v", "ms", "", "MK", T.MK[:], 1.0)
+        for ii in range(NB):
+            vts("J16 qm MK", "MKs", T.MK[:, STARTS[ii]:STARTS[ii] + 16], T.J16[:, 0:16], T.qm[:], O.is_gt, par=True)
+        vts("MKs MK", "MB", T.MB[:], T.MK[:], -1.0e8, O.mult, 1.0e8, O.add)
+
+    XW = "X X2"
+    Xw = T.X[:, 0:W]
+    CNw = T.CN[:, 0:U]
+    CH = [(0, 64), (64, 128), (128, 192)]
+    XG2 = "Xg2.0 Xg2.1 Xg2.2"
+    D2 = [("PA", T.PA), ("PB", T.PB), ("PA", T.PA)]
+    CNT = [("PC", T.PC, 0), ("PC", T.PC, 64), ("PW", T.PW, 192)]
+
+    def replay_rows(t):
+        mm("RSL%d TR" % t, "PW", T.PW[:, 0:192], T.RSL[:, 128 * t:128 * t + 128], T.TR[:], True, True)
+        mm("IDh TR", "PC", T.PC[:, 192:384], T.IDh[:], T.TR[:], True, True)
+        act("PC", "TRf", T.TRf[:], T.PC[:, 192:384], AF.Copy, bias=float(CMID))
+
+    def trail_update(t, out, nm):
+        for c in range(3):
+            pn, P, o = CNT[c]
+            vts(pn + " thr", "smt", T.smt[:, 64 * c:64 * c + 64], P[:, o:o + 64], T.thr[:, t:t + 1], O.is_gt, par=True)
+        vtt("smt D", "tD", T.tD[:], T.smt[:], T.D[:], O.mult)
+        vtt("tD PK", nm, out, T.tD[:], T.PK[:, 192:384], O.add)
+
+    def g2(c):
+        act(XW + " TRu", "Xg2.%d" % c, T.Xg2[:, 1024 * c:1024 * c + 1024], Xw.indirect(T.TRu[:, 64 * c:64 * c + 64]))
+
+    def diff(c, Zk):
+        nm, P = D2[c]
+        for k in range(16):
+            mm("IDb " + Zk, nm, P[:, 64 * k:64 * k + 64], T.IDb[:], T[Zk][:, 64 * c:64 * c + 64], True, False)
+            mm("NIb Xg2.%d" % c, nm, P[:, 64 * k:64 * k + 64], T.NIb[:], T.Xg2[:, 1024 * c + k:1024 * c + 1024:16], False, True)
+
+    def absd(c):
+        nm, P = D2[c]
+        act(nm, "A2.%d" % c, T.A2[:, c, :], P[:], AF.Abs)
+
+    def thr(c):
+        vts("A2.%d LIM" % c, "IND.%d" % c, T.IND[:, c, :], T.A2[:, c, :], T.LIM[:], O.is_gt)
+
+    def count(c):
+        nm, P, o = CNT[c]
+        for k in range(16):
+            mm("PD1 IND.%d" % c, nm, P[:, o:o + 64], T.PD1[:, 15 - k:143 - k], T.IND[:, c, 64 * k:64 * k + 64], k == 0, k == 15)
+
+    def ttmax(c):
+        lo, hi = CH[c]
+        for k in range(16):
+            vtt("Xg1.%d PZ" % c, "M1.%d" % c, T.M1[:, 4 * c:4 * c + 4, k::16], T.Xg1[:, 1024 * c + k:1024 * c + 1024:16],
+                T.PZ[:, lo:hi], O.max, par=True)
+
+    def score(c):
+        lo, hi = CH[c]
+        for p in range(16):
+            mm("PDN M1.%d" % c, "PK", T.PK[:, lo:hi], T.PDN[:, 15 - p:143 - p], T.M1[:, 4 * c:4 * c + 4, 16 * p:16 * p + 16],
+               False, c == 2 and p == 15)
+
+    outs = []
+
+    def fin(j):
+        c0 = 1536 * j
+        if j:
+            act(XW, "xo1", T.xraw[:, c0:c0 + 1536], T.X[:, c0:c0 + 1536], AF.Copy, bias=-float(XB))
+        else:
+            vts(XW, "xo0", T.xraw[:, c0:c0 + 1536], T.X[:, c0:c0 + 1536], -float(XB), O.add)
+        q = "sa"[j]
+        outs.append((q, dma(q, "xo%d" % j, "yx%d" % j, T.yx[:, c0:c0 + 1536], T.xraw[:, c0:c0 + 1536])))
+
+    for t in range(T_STEPS):
+        r = ROWS[t]
+        last = t == T_STEPS - 1
+        Zk = "Z%d" % t
+        Z = T[Zk]
+        vtc("CN VH", "Ku", T.Ku[:], CNw.indirect(T.VH[:]))
+        act("CN VH", "Kf", T.Kf[:], CNw.indirect(T.VH[:]), AF.Copy, bias=-float(CMID))
+        for c in (1, 2):
+            act(XW + " Ku", "Xg1.%d" % c, T.Xg1[:, 1024 * c:1024 * c + 1024], Xw.indirect(T.Ku[:, 64 * c:64 * c + 64]))
+        vtc(XW + " Ku", "Xg1.0", T.Xg1[:, 0:1024], Xw.indirect(T.Ku[:, 0:64]))
+        if not t:
+            consts_a()
+        else:
+            trail_update(t - 1, T.TR[:], "TR")
+            vts("TR", "TRu", T.TRu[:], T.TR[:], float(CMID), O.add)
+        mm("IDb " + Zk, "PZ", T.PZ[:, 0:192], T.IDb[:], Z[:], True, True)
+        replay_rows(t)
+        mm("BOb zero", "PK", T.PK[:, 0:192], T.BOb[:], T.zero[:], True, False)
+        ttmax(0)
+        score(0)
+        if not t:
+            consts_b()
+        for q in range(2):
+            vtc("Kf", "Kp", T.Kp[:, :, 16 * q:16 * q + 16], T.Kf[:, 96 * q:96 * q + 96], par=True)
+        op("v", "tr", "Kp", "V", T.V[:], T.Kp[:])
+        for q in range(2):
+            for h in range(2):
+                mm("V " + SWPS, "PK", T.PK[:, 96 * q:96 * q + 96], T.SWP[:, 256 * h + 128 * q:256 * h + 128 * q + 128],
+                   T.V[:, :, 16 * h:16 * h + 16], False, False)
+        g2(0)
+        ttmax(1)
+        score(1)
+        ttmax(2)
+        score(2)
+        if not t:
+            consts_c()
+        vtt("PW DM", "WD", T.WD[:], T.PW[:, 0:192], T.DM[:], O.mult)
+        op("v", "scan", "A0 WD", "WS", T.WS[:], T.A0[:], T.WD[:], 0.0, O.mult, O.add)
+        vts("WS", "wi", T.wu[:, 0:12], T.WS[:, 15::16], float(CMID), O.add)
+        vts("wi", "ui", T.wu[:, 12:24], T.wu[:, 0:12], 1, O.arith_shift_right)
+        vts("ui", "wb", T.wb[:], T.wu[:, 12:24], -2.0, O.mult, float(CMID) - 0.5, O.add)
+        vtc("ui", "LU", T.LU[:], T.wu[:, 12:24])
+        g2(1)
+        diff(0, Zk)
+        g2(2)
+        op("v", "scan", "RST PK", "Sc", T.Sc[:], T.RST[:], T.PK[:, 0:192], 0.0, O.max, O.min)
+        vts("Sc", "ci", T.ci[:], T.Sc[:, 15::16], float(CMID), O.add)
+        vts("ci", "cm", T.cm[:], T.ci[:], 4095, O.bitwise_and)
+        vts("cm", "cf", T.cf[:], T.cm[:], -float(CMID), O.add)
+        vtc("cm", "CL", T.CL[:], T.cm[:])
+        vtt("cf RP DM", "Dg", T.Dg[:], T.cf[:].indirect(T.RP[:]), T.DM[:], O.mult)
+        if not last:
+            vtt(XW + " CL " + Zk, "sg", T.sg[:], Xw.indirect(T.CL[:]), Z[:], O.add)
+        vts("IDf nrowm", "IDm%d" % t, T.IDm[:, 128 * t:128 * t + 128], T.IDf[:], T.nrowm[:, t:t + 1], O.mult)
+        mm("BOh Dg", "PZ", T.PZ[:, 192:384], T.BOh[:], T.Dg[:], True, True)
+        mm("IDm%d TR" % t, "PK", T.PK[:, 192:384], T.IDm[:, 128 * t:128 * t + 128], T.TR[:], True, False)
+        mm("PDH Dg", "PK", T.PK[:, 192:384], T.PDH[:, 15 - t:143 - t], T.Dg[:], False, True)
+        if not last:
+            vts("sg", "ZN%d" % t, T["ZN%d" % t][:], T.sg[:], 0.5, O.mult, -0.25, O.add)
+            dst = T.cores[(rank + 1 + t % (N - 1)) % N]
+            rid, pid, _e = topo.addr(dst)
+            need("g", wr["ZN%d" % t][0], wr["ZN%d" % t][1])
+            g.remote_dma(T["Z%d" % (t + 1)][:], T["ZN%d" % t][:], T.sem["zs%d" % (t + 1)], T.sem.zsent, pid, rid, topo.mask(core, dst))
+            src = T.cores[(rank - 1 - t % (N - 1)) % N]
+            note("zs%d" % (t + 1), len(topo.engines(src, core)), [], ["Z%d" % (t + 1)])
+            vts("cm", "ch", T.ch[:], T.cm[:], 1, O.arith_shift_right)
+            vtc("ch", "VH", T.VH[:], T.ch[:])
+        mm("IDb " + Zk, "PW", T.PW[:, 256:448], T.IDb[:], Z[:], True, False)
+        mm("NIb " + XG2, "PW", T.PW[:, 256:448], T.NIb[:], T.Xg2[:, r::16], False, True)
+        act("CN LU", "Co", T.Co[:], CNw.indirect(T.LU[:]), AF.Copy, bias=-float(CMID))
+        act("PW", "AR", T.AR[:], T.PW[:, 256:448], AF.Abs)
+        absd(0)
+        vtt("Kf PC", "D", T.D[:], T.Kf[:], T.PC[:, 192:384], O.subtract)
+        vtt("Co PC", "CG", T.CG[:], T.Co[:], T.PC[:, 192:384], O.subtract)
+        if t:
+            vtc("Sa", "Si", T.Si[:], T.Sa[:])
+            vts("Si", "Sj", T.Sj[:], T.Si[:], 3, O.bitwise_and)
+            vts("Sj", "LIM", T.LIM[:], T.Sj[:], 18.5, O.add)
+        if not last:
+            vts("BOf rowm", "RSL%d" % (t + 1), T.RSL[:, 128 * t + 128:128 * t + 256], T.BOf[:], T.rowm[:, ROWS[t + 1]:ROWS[t + 1] + 1], O.mult)
+        if not t:
+            consts_d()
+        vtc("PZ", "ACh", T.ACh[:], T.PZ[:, 192:384])
+        vts("AR LIM", "IR", T.IR[:], T.AR[:], T.LIM[:], O.is_gt)
+        for ii in range(NB):
+            vts("ACh cf", "E", T.E[:, STARTS[ii]:STARTS[ii + 1]], T.ACh[:, 16 * ii:192], T.cf[:, ii:ii + 1], O.is_equal, par=True)
+        for ii in range(NB):
+            act("PW wb", "SQ", T.SQ[:, STARTS[ii]:STARTS[ii + 1]], T.PW[:, 16 * ii:192], AF.Square, bias=T.wb[:, ii:ii + 1], par=True)
+        mm("IDb " + XG2, "PZ", T.PZ[:, 192:384], T.IDb[:], T.Xg2[:, r::16], True, False)
+        mm("IDb " + Zk, "PZ", T.PZ[:, 192:384], T.IDb[:], Z[:], False, True)
+        diff(1, Zk)
+        act("PZ", "H", T.H[:], T.PZ[:, 192:384], AF.Copy, scale=0.5, bias=-0.25)
+        act(XW + " CL", "xcut", T.xcut[:], Xw.indirect(T.CL[:]), AF.Copy, scale=0.5, bias=XB / 2 - 0.25)
+        absd(1)
+        op("v", "scan", "E MK MKs", "EC", T.EC[:], T.E[:], T.MK[:], 0.0, O.max, O.mult)
+        thr(0)
+        vts(XG2, "Q", T.Q[:], T.Xg2[:, r::16], 4.0, O.add, XB + 63.0, O.min)
+        mm("BOb IR", "PC", T.PC[:, 192:384], T.BOb[:], T.IR[:], True, True)
+        for p in range(16):
+            mm("PD1 IR", "PC", T.PC[:, 384:396], T.PD1[:, 15 - p:143 - p], T.IR[:, p::16], p == 0, p == 15)
+        mm("IDb Q", "PZ", T.PZ[:, 0:192], T.IDb[:], T.Q[:], True, False)
+        mm("NIb H", "PZ", T.PZ[:, 0:192], T.NIb[:], T.H[:], False, True)
+        diff(2, Zk)
+        op("v", "scan", "SQ MB", "SW", T.SW[:], T.SQ[:], T.MB[:], 1.0e8, O.min, O.max)
+        vtt("EC ENDS DUM", "ULf", T.ULf[:], T.EC[:].indirect(T.ENDS[:, 0:1]), T.DUM[:, 0:16], O.mult)
+        vts("SW ENDS", "NF", T.NF[:], T.SW[:].indirect(T.ENDS[:]), 1.0, O.is_lt)
+        vtt("ULf cm", "ULg", T.ULf[:, 0:12], T.ULf[:, 0:12], T.cm[:], O.max)
+        vtt("NF DUM", "e1", T.e1[:], T.NF[:, 0:24], T.DUM[:, 0:24], O.mult)
+        vtc("ULg", "UL", T.UL[:], T.ULf[:, 0:12])
+        vtt("e1 wi ui", "WU", T.WU[:], T.e1[:], T.wu[:], O.max)
+        vts("PC", "skr", T.skr[:], T.PC[:, 192:384], 8.5, O.is_gt)
+        vts("PC", "skb", T.skb[:], T.PC[:, 384:396], 8.5, O.is_gt, 2048.0, O.mult)
+        vtc("WU", "LH", T.LH[:], T.WU[:, 0:12])
+        count(0)
+        thr(1)
+        count(1)
+        absd(2)
+        vtt("skr PZ", "mQ", T.mQ[:], T.skr[:], T.PZ[:, 0:192], O.mult)
+        vtt("skb WU", "LCf", T.LCf[:], T.skb[:], T.WU[:, 12:24], O.add)
+        vtt("mQ H LH", XW, T.X[:].indirect(T.LH[:]), T.mQ[:], T.H[:], O.add)
+        vtc("LCf", "LC", T.LC[:], T.LCf[:])
+        vtc("xcut UL", XW, T.X[:].indirect(T.UL[:]), T.xcut[:])
+        if not last:
+            mm("onb skb", "PC", T.PC[:, 400:412], T.ONS[:], T.skb[:], True, True)
+            act("PC", "jnk Sa", T.jnk[:], T.PC[:, 400:412], AF.Copy, accum_out=T.Sa[:])
+        else:
+            for j in range(2):
+                fin(j)
+        thr(2)
+        count(2)
+        vts("PC", "sm0", T.sm[:, 0:128], T.PC[:, 0:128], 8.5, O.is_gt)
+        vtt("sm0 CG", "cD0", T.cD[:, 0:128], T.sm[:, 0:128], T.CG[:, 0:128], O.mult)
+        vts("PW", "sm1", T.sm[:, 128:192], T.PW[:, 192:256], 8.5, O.is_gt)
+        vtt("sm1 CG", "cD1", T.cD[:, 128:192], T.sm[:, 128:192], T.CG[:, 128:192], O.mult)
+        vtt("cD0 cD1 TRf LC", "CN", T.CN[:].indirect(T.LC[:]), T.cD[:], T.TRf[:], O.add)
+    for j in range(2):
+        q = "sa"[j]
+        outs.append((q, dma(q, "CN", "yl%d" % j, T.yl[:, 768 * j:768 * j + 768], T.CN[:, 768 * j:768 * j + 768])))
+    trail_update(T_STEPS - 1, T.TF[:], "TF")
+    vts("TF REV", "go", T.sg[:], T.TF[:].indirect(T.REV[:]), float(CMID), O.add)
+    outs.append(("s", dma("s", "go", "yg", T.yg[:], T.sg[:])))
+    for q, s in outs:
+        need(q, s, 16)
+    g.wait_ge(T.sem.zsent, sum(len(topo.engines(core, T.cores[(rank + 1 + t % (N - 1)) % N])) for t in range(T_STEPS - 1)))

@@ -22,11 +22,12 @@ _S = {
     "SQ": ([128, RUN], b16), "SW": ([128, RUN], b16), "NF": ([128, 32], f32), "e1": ([128, 24], f32), "WU": ([128, 24], f32),
     "LH": ([128, NB], u16), "LCf": ([128, NB], f32), "LC": ([128, NB], u16), "skb": ([128, NB], b16), "skr": ([128, B], b16),
     "H": ([128, B], b16), "Q": ([128, B], b16), "mQ": ([128, B], b16),
-    "D": ([128, B], f32), "sm": ([128, B], f32), "smt": ([128, B], f32), "tD": ([128, B], f32), "TRf": ([128, B], f32),
+    "sm": ([128, B], f32), "tD": ([128, B], f32), "TRf": ([128, B], f32),
     "Co": ([128, B], f32), "CG": ([128, B], f32), "cD": ([128, B], f32), "TF": ([128, B], f32),
-    "jnk": ([128, NB], f32), "Sa": ([128, 1], f32), "Si": ([128, 1], i32), "Sj": ([128, 1], i32), "LIM": ([128, 1], f32),
-    "qi": ([128, 1], i32), "qa": ([128, 1], i32), "qm": ([128, 1], f32), "rowm": ([128, 16], f32), "nrowm": ([128, 16], f32),
-    "thr": ([128, 16], f32), "half": ([128, 2], f32), "io1": ([128, 48], f32), "io2": ([128, 48], f32), "io3": ([128, 48], f32),
+    "jnk": ([128, NB], f32), "Sa": ([128, 1], f32), "Si": ([128, 1], i32), "Sj": ([128, 1], i32),
+    "LIM": ([128, 1], f32), "LB": ([128, 1], f32), "CB": ([128, 1], f32),
+    "qi": ([128, 1], i32), "qa": ([128, 1], i32), "qm": ([128, 1], f32),
+    "half": ([128, 2], f32), "io1": ([128, 48], f32), "io2": ([128, 48], f32), "io3": ([128, 48], f32),
     "REV": ([128, NB], u16), "RP": ([128, NB], u16), "ENDS": ([128, 2], u16), "DUM": ([128, 32], f32),
     "J16": ([128, B], f32), "DM": ([128, B], f32), "RST": ([128, B], f32), "A0": ([128, B], f32), "MK": ([128, RUN], b16), "MB": ([128, RUN], b16),
     "on": ([128, 144], f32), "on2": ([128, 144], f32), "BOf": ([128, 128], f32), "IDf": ([128, 128], f32), "sh0": ([128, 128], f32), "sh1": ([128, 128], f32),
@@ -160,9 +161,6 @@ def rank_program(g, core, T, topo):
     vts("io2", "REV", T.REV[:], T.io2[:, 0:12], -1.0, O.mult, 191.0, O.add)
     vts("J16", "A0", T.A0[:], T.J16[:], 0.0, O.not_equal)
     vtc("BOf", "BOh", T.BOh[:], T.BOf[:])
-    vts("J16 qm", "rowm", T.rowm[:], T.J16[:, 0:16], T.qm[:], O.is_equal)
-    vts("J16 qm", "nrowm", T.nrowm[:], T.J16[:, 0:16], T.qm[:], O.not_equal)
-    vts("rowm", "thr", T.thr[:], T.rowm[:], 1000.0, O.mult, 8.5, O.add)
     vts("io1", "RP", T.RP[:], T.io1[:, 0:12], 0.0625, O.mult)
     vts("J16 qm", "IDf0", T.IDf[:], T.J16[:, 0:128], T.qm[:], O.is_equal)
     vtt("IDf0 BOf", "IDf", T.IDf[:], T.IDf[:], T.BOf[:], O.mult)
@@ -171,6 +169,10 @@ def rank_program(g, core, T, topo):
     act("on2", "PDN", T.PDN[:], T.on2[:], AF.Copy, scale=-4096.0)
     act("BOf", "BOb", T.BOb[:], T.BOf[:])
     act("zraw REV", "Z0", T.Z0[:], T.zraw[:].indirect(T.REV[:]), AF.Copy, bias=float(XB))
+    vtc("IDf", "IDh", T.IDh[:], T.IDf[:])
+    for m in range(T_STEPS):
+        op("g", "sel", "BOh", "RSL%d" % m, T.RSL[:, 128 * m:128 * m + 128], T.BOh[:], [[-16, 8], [0, 16]], O.is_equal, 0.0, -ROWS[m], 1)
+        op("g", "sel", "IDh", "IDm%d" % m, T.IDm[:, 128 * m:128 * m + 128], T.IDh[:], [[0, 8], [1, 16]], O.not_equal, 0.0, -m, 0)
     vts("vraw " + VR, "vsh", T.vsh[:], T.vraw[:], 1, O.arith_shift_right)
     vtc("vsh", "vfh", T.vfh[:], T.vsh[:])
     mm("BOh vfh", "PW", T.PW[:, 0:192], T.BOh[:], T.vfh[:], True, True)
@@ -186,21 +188,24 @@ def rank_program(g, core, T, topo):
     act("on2", "PD1", T.PD1[:], T.on2[:])
     SWPS = "SWP00 SWP01 SWP10 SWP11"
 
+    def trail_list(j):
+        lo, hi = ((0, 128), (128, 192))[j]
+        vts("TR%d" % j, "TRu%d" % j, T.TRu[:, lo:hi], T.TR[:, lo:hi], float(CMID), O.add)
+
     def consts_a():
-        vts("traw REV", "TR", T.TR[:], T.traw[:].indirect(T.REV[:]), -float(CMID), O.add)
-        vts("TR", "TRu", T.TRu[:], T.TR[:], float(CMID), O.add)
-        vtc("IDf", "IDh", T.IDh[:], T.IDf[:])
-        vts("BOf rowm", "RSL0", T.RSL[:, 0:128], T.BOf[:], T.rowm[:, ROWS[0]:ROWS[0] + 1], O.mult)
+        vts("traw REV", "TR0 TR1", T.TR[:], T.traw[:].indirect(T.REV[:]), -float(CMID), O.add)
+        trail_list(0)
+        trail_list(1)
         op("v", "ms", "", "zero", T.zero[:], 0.0)
 
     def consts_b():
         vts("qi", "Si", T.Si[:], T.qi[:], 16, O.bitwise_and)
         vts("Si", "half", T.half[:, 1:2], T.Si[:], 0.0625, O.mult)
         vts("half", "half0", T.half[:, 0:1], T.half[:, 1:2], -1.0, O.mult, 1.0, O.add)
-        vts("IDf half half0", "SWP00", T.SWP[:, 0:128], T.IDf[:], T.half[:, 0:1], O.mult)
-        vts("sh0 half half0", "SWP10", T.SWP[:, 256:384], T.sh0[:], T.half[:, 0:1], O.mult)
-        vts("sh1 half half0", "SWP01", T.SWP[:, 128:256], T.sh1[:], T.half[:, 1:2], O.mult)
-        vts("IDf half half0", "SWP11", T.SWP[:, 384:512], T.IDf[:], T.half[:, 1:2], O.mult)
+        vts("IDf half half0", "SWP00", T.SWP[:, 0:128], T.IDf[:], T.half[:, 0:1], O.mult, -1.0, O.mult)
+        vts("sh0 half half0", "SWP10", T.SWP[:, 256:384], T.sh0[:], T.half[:, 0:1], O.mult, -1.0, O.mult)
+        vts("sh1 half half0", "SWP01", T.SWP[:, 128:256], T.sh1[:], T.half[:, 1:2], O.mult, -1.0, O.mult)
+        vts("IDf half half0", "SWP11", T.SWP[:, 384:512], T.IDf[:], T.half[:, 1:2], O.mult, -1.0, O.mult)
 
     def consts_c():
         vts("J16", "RST0", T.RST[:], T.J16[:], 0.0, O.is_equal, 2.0e8, O.mult)
@@ -218,6 +223,7 @@ def rank_program(g, core, T, topo):
         vts("io3", "ENDS", T.ENDS[:], T.io3[:, 4:6], -1.0, O.add)
         vtc("on2", "PDH", T.PDH[:], T.on2[:])
         op("v", "ms", "", "LIM", T.LIM[:], 18.5)
+        op("v", "ms", "", "CB", T.CB[:], -1700.0)
 
     def consts_d():
         op("v", "ms", "", "onb", T.ONS[:], 1.0 / 2048.0)
@@ -232,26 +238,24 @@ def rank_program(g, core, T, topo):
     CH = [(0, 64), (64, 128), (128, 192)]
     XG2 = "Xg2.0 Xg2.1 Xg2.2"
     D2 = [("PA", T.PA), ("PB", T.PB), ("PA", T.PA)]
-    CNT = [("PC", T.PC, 0), ("PC", T.PC, 64), ("PW", T.PW, 192)]
+    CNT = [("PC", T.PC, 0), ("PC", T.PC, 64), ("PB", T.PB, 0)]
 
     def replay_rows(t):
-        mm("RSL%d TR" % t, "PW", T.PW[:, 0:192], T.RSL[:, 128 * t:128 * t + 128], T.TR[:], True, True)
-        mm("IDh TR", "PC", T.PC[:, 192:384], T.IDh[:], T.TR[:], True, True)
+        mm("RSL%d TR0 TR1" % t, "PW", T.PW[:, 0:192], T.RSL[:, 128 * t:128 * t + 128], T.TR[:], True, True)
+        mm("IDh TR0 TR1", "PC", T.PC[:, 192:384], T.IDh[:], T.TR[:], True, True)
         act("PC", "TRf", T.TRf[:], T.PC[:, 192:384], AF.Copy, bias=float(CMID))
 
-    def trail_update(t, out, nm):
-        for c in range(3):
-            pn, P, o = CNT[c]
-            vts(pn + " thr", "smt", T.smt[:, 64 * c:64 * c + 64], P[:, o:o + 64], T.thr[:, t:t + 1], O.is_gt, par=True)
-        vtt("smt D", "tD", T.tD[:], T.smt[:], T.D[:], O.mult)
-        vtt("tD PK", nm, out, T.tD[:], T.PK[:, 192:384], O.add)
+    def trail_part(j, out, nm):
+        lo, hi = ((0, 128), (128, 192))[j]
+        vtt("sm%d PW" % j, "tD%d" % j, T.tD[:, lo:hi], T.sm[:, lo:hi], T.PW[:, 256 + lo:256 + hi], O.mult)
+        vtt("tD%d PK" % j, nm + "%d" % j, out[:, lo:hi], T.PK[:, 192 + lo:192 + hi], T.tD[:, lo:hi], O.subtract)
 
     def g2(c):
-        act(XW + " TRu", "Xg2.%d" % c, T.Xg2[:, 1024 * c:1024 * c + 1024], Xw.indirect(T.TRu[:, 64 * c:64 * c + 64]))
+        act(XW + " TRu%d" % (c // 2), "Xg2.%d" % c, T.Xg2[:, 1024 * c:1024 * c + 1024], Xw.indirect(T.TRu[:, 64 * c:64 * c + 64]))
 
-    def diff(c, Zk):
+    def diff(c, Zk, k0=0, k1=16):
         nm, P = D2[c]
-        for k in range(16):
+        for k in range(k0, k1):
             mm("IDb " + Zk, nm, P[:, 64 * k:64 * k + 64], T.IDb[:], T[Zk][:, 64 * c:64 * c + 64], True, False)
             mm("NIb Xg2.%d" % c, nm, P[:, 64 * k:64 * k + 64], T.NIb[:], T.Xg2[:, 1024 * c + k:1024 * c + 1024:16], False, True)
 
@@ -293,7 +297,7 @@ def rank_program(g, core, T, topo):
     for t in range(T_STEPS):
         r = ROWS[t]
         last = t == T_STEPS - 1
-        Zk = "Z%d" % t
+        Zk, Zn = "Z%d" % t, "Z%d" % (t + 1)
         Z = T[Zk]
         vtc("CN VH", "Ku", T.Ku[:], CNw.indirect(T.VH[:]))
         act("CN VH", "Kf", T.Kf[:], CNw.indirect(T.VH[:]), AF.Copy, bias=-float(CMID))
@@ -302,10 +306,13 @@ def rank_program(g, core, T, topo):
         vtc(XW + " Ku", "Xg1.0", T.Xg1[:, 0:1024], Xw.indirect(T.Ku[:, 0:64]))
         if not t:
             consts_a()
+            mm("IDb " + Zk, "PZ", T.PZ[:, 0:192], T.IDb[:], Z[:], True, True)
         else:
-            trail_update(t - 1, T.TR[:], "TR")
-            vts("TR", "TRu", T.TRu[:], T.TR[:], float(CMID), O.add)
-        mm("IDb " + Zk, "PZ", T.PZ[:, 0:192], T.IDb[:], Z[:], True, True)
+            trail_part(1, T.TR[:], "TR")
+            trail_list(1)
+            vtc("Sa", "Si", T.Si[:], T.Sa[:])
+            vts("Si", "Sj", T.Sj[:], T.Si[:], 3, O.bitwise_and)
+            vts("Sj", "LIM", T.LIM[:], T.Sj[:], 18.5, O.add)
         replay_rows(t)
         mm("BOb zero", "PK", T.PK[:, 0:192], T.BOb[:], T.zero[:], True, False)
         ttmax(0)
@@ -313,17 +320,24 @@ def rank_program(g, core, T, topo):
         if not t:
             consts_b()
         for q in range(2):
-            vtc("Kf", "Kp", T.Kp[:, :, 16 * q:16 * q + 16], T.Kf[:, 96 * q:96 * q + 96], par=True)
+            vts("Kf", "Kp", T.Kp[:, :, 16 * q:16 * q + 16], T.Kf[:, 96 * q:96 * q + 96], -1.0, O.mult, par=True)
         op("v", "tr", "Kp", "V", T.V[:], T.Kp[:])
         for q in range(2):
             for h in range(2):
                 mm("V " + SWPS, "PK", T.PK[:, 96 * q:96 * q + 96], T.SWP[:, 256 * h + 128 * q:256 * h + 128 * q + 128],
                    T.V[:, :, 16 * h:16 * h + 16], False, False)
-        g2(0)
+        if not t:
+            for c in range(2):
+                g2(c)
+                diff(c, Zk)
+        absd(0)
+        g2(2)
+        absd(1)
         ttmax(1)
         score(1)
         ttmax(2)
         score(2)
+        diff(2, Zk, 0, 8)
         if not t:
             consts_c()
         vtt("PW DM", "WD", T.WD[:], T.PW[:, 0:192], T.DM[:], O.mult)
@@ -332,9 +346,7 @@ def rank_program(g, core, T, topo):
         vts("wi", "ui", T.wu[:, 12:24], T.wu[:, 0:12], 1, O.arith_shift_right)
         vts("ui", "wb", T.wb[:], T.wu[:, 12:24], -2.0, O.mult, float(CMID) - 0.5, O.add)
         vtc("ui", "LU", T.LU[:], T.wu[:, 12:24])
-        g2(1)
-        diff(0, Zk)
-        g2(2)
+        thr(0)
         op("v", "scan", "RST PK", "Sc", T.Sc[:], T.RST[:], T.PK[:, 0:192], 0.0, O.max, O.min)
         vts("Sc", "ci", T.ci[:], T.Sc[:, 15::16], float(CMID), O.add)
         vts("ci", "cm", T.cm[:], T.ci[:], 4095, O.bitwise_and)
@@ -343,56 +355,52 @@ def rank_program(g, core, T, topo):
         vtt("cf RP DM", "Dg", T.Dg[:], T.cf[:].indirect(T.RP[:]), T.DM[:], O.mult)
         if not last:
             vtt(XW + " CL " + Zk, "sg", T.sg[:], Xw.indirect(T.CL[:]), Z[:], O.add)
-        vts("IDf nrowm", "IDm%d" % t, T.IDm[:, 128 * t:128 * t + 128], T.IDf[:], T.nrowm[:, t:t + 1], O.mult)
         mm("BOh Dg", "PZ", T.PZ[:, 192:384], T.BOh[:], T.Dg[:], True, True)
-        mm("IDm%d TR" % t, "PK", T.PK[:, 192:384], T.IDm[:, 128 * t:128 * t + 128], T.TR[:], True, False)
+        mm("IDm%d TR0 TR1" % t, "PK", T.PK[:, 192:384], T.IDm[:, 128 * t:128 * t + 128], T.TR[:], True, False)
         mm("PDH Dg", "PK", T.PK[:, 192:384], T.PDH[:, 15 - t:143 - t], T.Dg[:], False, True)
         if not last:
             vts("sg", "ZN%d" % t, T["ZN%d" % t][:], T.sg[:], 0.5, O.mult, -0.25, O.add)
             dst = T.cores[(rank + 1 + t % (N - 1)) % N]
             rid, pid, _e = topo.addr(dst)
             need("g", wr["ZN%d" % t][0], wr["ZN%d" % t][1])
-            g.remote_dma(T["Z%d" % (t + 1)][:], T["ZN%d" % t][:], T.sem["zs%d" % (t + 1)], T.sem.zsent, pid, rid, topo.mask(core, dst))
+            g.remote_dma(T[Zn][:], T["ZN%d" % t][:], T.sem["zs%d" % (t + 1)], T.sem.zsent, pid, rid, topo.mask(core, dst))
             src = T.cores[(rank - 1 - t % (N - 1)) % N]
-            note("zs%d" % (t + 1), len(topo.engines(src, core)), [], ["Z%d" % (t + 1)])
+            note("zs%d" % (t + 1), len(topo.engines(src, core)), [], [Zn])
             vts("cm", "ch", T.ch[:], T.cm[:], 1, O.arith_shift_right)
             vtc("ch", "VH", T.VH[:], T.ch[:])
-        mm("IDb " + Zk, "PW", T.PW[:, 256:448], T.IDb[:], Z[:], True, False)
-        mm("NIb " + XG2, "PW", T.PW[:, 256:448], T.NIb[:], T.Xg2[:, r::16], False, True)
         act("CN LU", "Co", T.Co[:], CNw.indirect(T.LU[:]), AF.Copy, bias=-float(CMID))
-        act("PW", "AR", T.AR[:], T.PW[:, 256:448], AF.Abs)
-        absd(0)
-        vtt("Kf PC", "D", T.D[:], T.Kf[:], T.PC[:, 192:384], O.subtract)
         vtt("Co PC", "CG", T.CG[:], T.Co[:], T.PC[:, 192:384], O.subtract)
-        if t:
-            vtc("Sa", "Si", T.Si[:], T.Sa[:])
-            vts("Si", "Sj", T.Sj[:], T.Si[:], 3, O.bitwise_and)
-            vts("Sj", "LIM", T.LIM[:], T.Sj[:], 18.5, O.add)
-        if not last:
-            vts("BOf rowm", "RSL%d" % (t + 1), T.RSL[:, 128 * t + 128:128 * t + 256], T.BOf[:], T.rowm[:, ROWS[t + 1]:ROWS[t + 1] + 1], O.mult)
+        mm("IDb " + Zk, "PK", T.PK[:, 0:192], T.IDb[:], Z[:], True, False)
+        mm("NIb " + XG2, "PK", T.PK[:, 0:192], T.NIb[:], T.Xg2[:, r::16], False, True)
+        act("PK", "AR", T.AR[:], T.PK[:, 0:192], AF.Abs)
         if not t:
             consts_d()
         vtc("PZ", "ACh", T.ACh[:], T.PZ[:, 192:384])
-        vts("AR LIM", "IR", T.IR[:], T.AR[:], T.LIM[:], O.is_gt)
         for ii in range(NB):
             vts("ACh cf", "E", T.E[:, STARTS[ii]:STARTS[ii + 1]], T.ACh[:, 16 * ii:192], T.cf[:, ii:ii + 1], O.is_equal, par=True)
-        for ii in range(NB):
-            act("PW wb", "SQ", T.SQ[:, STARTS[ii]:STARTS[ii + 1]], T.PW[:, 16 * ii:192], AF.Square, bias=T.wb[:, ii:ii + 1], par=True)
         mm("IDb " + XG2, "PZ", T.PZ[:, 192:384], T.IDb[:], T.Xg2[:, r::16], True, False)
         mm("IDb " + Zk, "PZ", T.PZ[:, 192:384], T.IDb[:], Z[:], False, True)
-        diff(1, Zk)
+        diff(2, Zk, 8, 16)
         act("PZ", "H", T.H[:], T.PZ[:, 192:384], AF.Copy, scale=0.5, bias=-0.25)
-        act(XW + " CL", "xcut", T.xcut[:], Xw.indirect(T.CL[:]), AF.Copy, scale=0.5, bias=XB / 2 - 0.25)
-        absd(1)
-        op("v", "scan", "E MK MKs", "EC", T.EC[:], T.E[:], T.MK[:], 0.0, O.max, O.mult)
-        thr(0)
+        for ii in range(NB):
+            act("PW wb", "SQ", T.SQ[:, STARTS[ii]:STARTS[ii + 1]], T.PW[:, 16 * ii:192], AF.Square, bias=T.wb[:, ii:ii + 1], par=True)
+        vts("AR LIM", "IR", T.IR[:], T.AR[:], T.LIM[:], O.is_gt)
         vts(XG2, "Q", T.Q[:], T.Xg2[:, r::16], 4.0, O.add, XB + 63.0, O.min)
         mm("BOb IR", "PC", T.PC[:, 192:384], T.BOb[:], T.IR[:], True, True)
         for p in range(16):
             mm("PD1 IR", "PC", T.PC[:, 384:396], T.PD1[:, 15 - p:143 - p], T.IR[:, p::16], p == 0, p == 15)
         mm("IDb Q", "PZ", T.PZ[:, 0:192], T.IDb[:], T.Q[:], True, False)
         mm("NIb H", "PZ", T.PZ[:, 0:192], T.NIb[:], T.H[:], False, True)
-        diff(2, Zk)
+        act(XW + " CL", "xcut", T.xcut[:], Xw.indirect(T.CL[:]), AF.Copy, scale=0.5, bias=XB / 2 - 0.25)
+        act("PC CB", "skr", T.skr[:], T.PC[:, 192:384], AF.Sigmoid, bias=T.CB[:], scale=200.0)
+        absd(2)
+        act("LIM", "LB", T.LB[:], T.LIM[:], AF.Copy, scale=-200.0)
+        act("A2.2 LB", "IND.2", T.IND[:, 2, :], T.A2[:, 2, :], AF.Sigmoid, bias=T.LB[:], scale=200.0)
+        op("v", "scan", "E MK MKs", "EC", T.EC[:], T.E[:], T.MK[:], 0.0, O.max, O.mult)
+        thr(1)
+        for q in range(2):
+            mm("IDm%d Kp" % t, "PW", T.PW[:, 256 + 96 * q:352 + 96 * q], T.IDm[:, 128 * t:128 * t + 128], T.Kp[:, :, 16 * q:16 * q + 16], True, False)
+            mm("IDm%d TR0 TR1" % t, "PW", T.PW[:, 256 + 96 * q:352 + 96 * q], T.IDm[:, 128 * t:128 * t + 128], T.TR[:, 96 * q:96 * q + 96], False, True)
         op("v", "scan", "SQ MB", "SW", T.SW[:], T.SQ[:], T.MB[:], 1.0e8, O.min, O.max)
         vtt("EC ENDS DUM", "ULf", T.ULf[:], T.EC[:].indirect(T.ENDS[:, 0:1]), T.DUM[:, 0:16], O.mult)
         vts("SW ENDS", "NF", T.NF[:], T.SW[:].indirect(T.ENDS[:]), 1.0, O.is_lt)
@@ -400,36 +408,42 @@ def rank_program(g, core, T, topo):
         vtt("NF DUM", "e1", T.e1[:], T.NF[:, 0:24], T.DUM[:, 0:24], O.mult)
         vtc("ULg", "UL", T.UL[:], T.ULf[:, 0:12])
         vtt("e1 wi ui", "WU", T.WU[:], T.e1[:], T.wu[:], O.max)
-        vts("PC", "skr", T.skr[:], T.PC[:, 192:384], 8.5, O.is_gt)
         vts("PC", "skb", T.skb[:], T.PC[:, 384:396], 8.5, O.is_gt, 2048.0, O.mult)
         vtc("WU", "LH", T.LH[:], T.WU[:, 0:12])
         count(0)
-        thr(1)
         count(1)
-        absd(2)
         vtt("skr PZ", "mQ", T.mQ[:], T.skr[:], T.PZ[:, 0:192], O.mult)
         vtt("skb WU", "LCf", T.LCf[:], T.skb[:], T.WU[:, 12:24], O.add)
         vtt("mQ H LH", XW, T.X[:].indirect(T.LH[:]), T.mQ[:], T.H[:], O.add)
         vtc("LCf", "LC", T.LC[:], T.LCf[:])
         vtc("xcut UL", XW, T.X[:].indirect(T.UL[:]), T.xcut[:])
+        if last:
+            for j in range(2):
+                fin(j)
+        vts("PC", "sm0", T.sm[:, 0:128], T.PC[:, 0:128], 8.5, O.is_gt)
         if not last:
             mm("onb skb", "PC", T.PC[:, 400:412], T.ONS[:], T.skb[:], True, True)
             act("PC", "jnk Sa", T.jnk[:], T.PC[:, 400:412], AF.Copy, accum_out=T.Sa[:])
-        else:
-            for j in range(2):
-                fin(j)
-        thr(2)
         count(2)
-        vts("PC", "sm0", T.sm[:, 0:128], T.PC[:, 0:128], 8.5, O.is_gt)
+        if not last:
+            trail_part(0, T.TR[:], "TR")
+            trail_list(0)
+            for c in range(2):
+                g2(c)
+            mm("IDb " + Zn, "PZ", T.PZ[:, 0:192], T.IDb[:], T[Zn][:], True, True)
+            diff(0, Zn)
         vtt("sm0 CG", "cD0", T.cD[:, 0:128], T.sm[:, 0:128], T.CG[:, 0:128], O.mult)
-        vts("PW", "sm1", T.sm[:, 128:192], T.PW[:, 192:256], 8.5, O.is_gt)
+        vts("PB", "sm1", T.sm[:, 128:192], T.PB[:, 0:64], 8.5, O.is_gt)
         vtt("sm1 CG", "cD1", T.cD[:, 128:192], T.sm[:, 128:192], T.CG[:, 128:192], O.mult)
         vtt("cD0 cD1 TRf LC", "CN", T.CN[:].indirect(T.LC[:]), T.cD[:], T.TRf[:], O.add)
+        if not last:
+            diff(1, Zn)
     for j in range(2):
         q = "sa"[j]
         outs.append((q, dma(q, "CN", "yl%d" % j, T.yl[:, 768 * j:768 * j + 768], T.CN[:, 768 * j:768 * j + 768])))
-    trail_update(T_STEPS - 1, T.TF[:], "TF")
-    vts("TF REV", "go", T.sg[:], T.TF[:].indirect(T.REV[:]), float(CMID), O.add)
+    for j in range(2):
+        trail_part(j, T.TF[:], "TF")
+    vts("TF0 TF1 REV", "go", T.sg[:], T.TF[:].indirect(T.REV[:]), float(CMID), O.add)
     outs.append(("s", dma("s", "go", "yg", T.yg[:], T.sg[:])))
     for q, s in outs:
         need(q, s, 16)

@@ -238,16 +238,19 @@ def rank_program(g, core, T, topo):
     CH = [(0, 64), (64, 128), (128, 192)]
     XG2 = "Xg2.0 Xg2.1 Xg2.2"
     D2 = [("PA", T.PA), ("PB", T.PB), ("PA", T.PA)]
-    CNT = [("PC", T.PC, 0), ("PC", T.PC, 64), ("PB", T.PB, 0)]
+    CNT = [("PB", T.PB, 0), ("PB", T.PB, 64), ("PC", T.PC, 0)]
 
     def replay_rows(t):
         mm("RSL%d TR0 TR1" % t, "PW", T.PW[:, 0:192], T.RSL[:, 128 * t:128 * t + 128], T.TR[:], True, True)
         mm("IDh TR0 TR1", "PC", T.PC[:, 192:384], T.IDh[:], T.TR[:], True, True)
         act("PC", "TRf", T.TRf[:], T.PC[:, 192:384], AF.Copy, bias=float(CMID))
 
-    def trail_part(j, out, nm):
+    def trail_a(j):
         lo, hi = ((0, 128), (128, 192))[j]
         vtt("sm%d PW" % j, "tD%d" % j, T.tD[:, lo:hi], T.sm[:, lo:hi], T.PW[:, 256 + lo:256 + hi], O.mult)
+
+    def trail_b(j, out, nm):
+        lo, hi = ((0, 128), (128, 192))[j]
         vtt("tD%d PK" % j, nm + "%d" % j, out[:, lo:hi], T.PK[:, 192 + lo:192 + hi], T.tD[:, lo:hi], O.subtract)
 
     def g2(c):
@@ -271,11 +274,13 @@ def rank_program(g, core, T, topo):
         for k in range(16):
             mm("PD1 IND.%d" % c, nm, P[:, o:o + 64], T.PD1[:, 15 - k:143 - k], T.IND[:, c, 64 * k:64 * k + 64], k == 0, k == 15)
 
-    def ttmax(c):
+    def ttmax(c, fill=()):
         lo, hi = CH[c]
         for k in range(16):
             vtt("Xg1.%d PZ" % c, "M1.%d" % c, T.M1[:, 4 * c:4 * c + 4, k::16], T.Xg1[:, 1024 * c + k:1024 * c + 1024:16],
                 T.PZ[:, lo:hi], O.max, par=True)
+            if k % 4 == 3 and k // 4 < len(fill):
+                fill[k // 4]()
 
     def score(c):
         lo, hi = CH[c]
@@ -308,50 +313,54 @@ def rank_program(g, core, T, topo):
             consts_a()
             mm("IDb " + Zk, "PZ", T.PZ[:, 0:192], T.IDb[:], Z[:], True, True)
         else:
-            trail_part(1, T.TR[:], "TR")
-            trail_list(1)
             vtc("Sa", "Si", T.Si[:], T.Sa[:])
+            trail_a(1)
             vts("Si", "Sj", T.Sj[:], T.Si[:], 3, O.bitwise_and)
+            trail_b(1, T.TR[:], "TR")
             vts("Sj", "LIM", T.LIM[:], T.Sj[:], 18.5, O.add)
+            trail_list(1)
         replay_rows(t)
         mm("BOb zero", "PK", T.PK[:, 0:192], T.BOb[:], T.zero[:], True, False)
         ttmax(0)
         score(0)
         if not t:
             consts_b()
-        for q in range(2):
-            vts("Kf", "Kp", T.Kp[:, :, 16 * q:16 * q + 16], T.Kf[:, 96 * q:96 * q + 96], -1.0, O.mult, par=True)
-        op("v", "tr", "Kp", "V", T.V[:], T.Kp[:])
-        for q in range(2):
-            for h in range(2):
-                mm("V " + SWPS, "PK", T.PK[:, 96 * q:96 * q + 96], T.SWP[:, 256 * h + 128 * q:256 * h + 128 * q + 128],
-                   T.V[:, :, 16 * h:16 * h + 16], False, False)
-        if not t:
             for c in range(2):
                 g2(c)
                 diff(c, Zk)
         absd(0)
         g2(2)
         absd(1)
-        ttmax(1)
+        fills = [
+            lambda: [vts("Kf", "Kp", T.Kp[:, :, 16 * q:16 * q + 16], T.Kf[:, 96 * q:96 * q + 96], -1.0, O.mult, par=True) for q in range(2)],
+            lambda: op("v", "tr", "Kp", "V", T.V[:], T.Kp[:]),
+            lambda: vtt("PW DM", "WD", T.WD[:], T.PW[:, 0:192], T.DM[:], O.mult),
+            lambda: op("v", "scan", "A0 WD", "WS", T.WS[:], T.A0[:], T.WD[:], 0.0, O.mult, O.add),
+            lambda: vts("WS", "wi", T.wu[:, 0:12], T.WS[:, 15::16], float(CMID), O.add),
+            lambda: vts("wi", "ui", T.wu[:, 12:24], T.wu[:, 0:12], 1, O.arith_shift_right),
+            lambda: vtc("ui", "LU", T.LU[:], T.wu[:, 12:24]),
+            lambda: vts("ui", "wb", T.wb[:], T.wu[:, 12:24], -2.0, O.mult, float(CMID) - 0.5, O.add)]
+        ttmax(1, fills[:4])
+        for q in range(2):
+            for h in range(2):
+                mm("V " + SWPS, "PK", T.PK[:, 96 * q:96 * q + 96], T.SWP[:, 256 * h + 128 * q:256 * h + 128 * q + 128],
+                   T.V[:, :, 16 * h:16 * h + 16], False, False)
         score(1)
-        ttmax(2)
+        ttmax(2, fills[4:])
         score(2)
         diff(2, Zk, 0, 8)
         if not t:
             consts_c()
-        vtt("PW DM", "WD", T.WD[:], T.PW[:, 0:192], T.DM[:], O.mult)
-        op("v", "scan", "A0 WD", "WS", T.WS[:], T.A0[:], T.WD[:], 0.0, O.mult, O.add)
-        vts("WS", "wi", T.wu[:, 0:12], T.WS[:, 15::16], float(CMID), O.add)
-        vts("wi", "ui", T.wu[:, 12:24], T.wu[:, 0:12], 1, O.arith_shift_right)
-        vts("ui", "wb", T.wb[:], T.wu[:, 12:24], -2.0, O.mult, float(CMID) - 0.5, O.add)
-        vtc("ui", "LU", T.LU[:], T.wu[:, 12:24])
         thr(0)
+        count(0)
         op("v", "scan", "RST PK", "Sc", T.Sc[:], T.RST[:], T.PK[:, 0:192], 0.0, O.max, O.min)
+        act("CN LU", "Co", T.Co[:], CNw.indirect(T.LU[:]), AF.Copy, bias=-float(CMID))
         vts("Sc", "ci", T.ci[:], T.Sc[:, 15::16], float(CMID), O.add)
         vts("ci", "cm", T.cm[:], T.ci[:], 4095, O.bitwise_and)
         vts("cm", "cf", T.cf[:], T.cm[:], -float(CMID), O.add)
         vtc("cm", "CL", T.CL[:], T.cm[:])
+        if not last:
+            vts("cm", "ch", T.ch[:], T.cm[:], 1, O.arith_shift_right)
         vtt("cf RP DM", "Dg", T.Dg[:], T.cf[:].indirect(T.RP[:]), T.DM[:], O.mult)
         if not last:
             vtt(XW + " CL " + Zk, "sg", T.sg[:], Xw.indirect(T.CL[:]), Z[:], O.add)
@@ -359,6 +368,7 @@ def rank_program(g, core, T, topo):
         mm("IDm%d TR0 TR1" % t, "PK", T.PK[:, 192:384], T.IDm[:, 128 * t:128 * t + 128], T.TR[:], True, False)
         mm("PDH Dg", "PK", T.PK[:, 192:384], T.PDH[:, 15 - t:143 - t], T.Dg[:], False, True)
         if not last:
+            vtc("ch", "VH", T.VH[:], T.ch[:])
             vts("sg", "ZN%d" % t, T["ZN%d" % t][:], T.sg[:], 0.5, O.mult, -0.25, O.add)
             dst = T.cores[(rank + 1 + t % (N - 1)) % N]
             rid, pid, _e = topo.addr(dst)
@@ -366,9 +376,6 @@ def rank_program(g, core, T, topo):
             g.remote_dma(T[Zn][:], T["ZN%d" % t][:], T.sem["zs%d" % (t + 1)], T.sem.zsent, pid, rid, topo.mask(core, dst))
             src = T.cores[(rank - 1 - t % (N - 1)) % N]
             note("zs%d" % (t + 1), len(topo.engines(src, core)), [], [Zn])
-            vts("cm", "ch", T.ch[:], T.cm[:], 1, O.arith_shift_right)
-            vtc("ch", "VH", T.VH[:], T.ch[:])
-        act("CN LU", "Co", T.Co[:], CNw.indirect(T.LU[:]), AF.Copy, bias=-float(CMID))
         vtt("Co PC", "CG", T.CG[:], T.Co[:], T.PC[:, 192:384], O.subtract)
         mm("IDb " + Zk, "PK", T.PK[:, 0:192], T.IDb[:], Z[:], True, False)
         mm("NIb " + XG2, "PK", T.PK[:, 0:192], T.NIb[:], T.Xg2[:, r::16], False, True)
@@ -398,6 +405,7 @@ def rank_program(g, core, T, topo):
         act("A2.2 LB", "IND.2", T.IND[:, 2, :], T.A2[:, 2, :], AF.Sigmoid, bias=T.LB[:], scale=200.0)
         op("v", "scan", "E MK MKs", "EC", T.EC[:], T.E[:], T.MK[:], 0.0, O.max, O.mult)
         thr(1)
+        count(1)
         for q in range(2):
             mm("IDm%d Kp" % t, "PW", T.PW[:, 256 + 96 * q:352 + 96 * q], T.IDm[:, 128 * t:128 * t + 128], T.Kp[:, :, 16 * q:16 * q + 16], True, False)
             mm("IDm%d TR0 TR1" % t, "PW", T.PW[:, 256 + 96 * q:352 + 96 * q], T.IDm[:, 128 * t:128 * t + 128], T.TR[:, 96 * q:96 * q + 96], False, True)
@@ -410,39 +418,42 @@ def rank_program(g, core, T, topo):
         vtt("e1 wi ui", "WU", T.WU[:], T.e1[:], T.wu[:], O.max)
         vts("PC", "skb", T.skb[:], T.PC[:, 384:396], 8.5, O.is_gt, 2048.0, O.mult)
         vtc("WU", "LH", T.LH[:], T.WU[:, 0:12])
-        count(0)
-        count(1)
         vtt("skr PZ", "mQ", T.mQ[:], T.skr[:], T.PZ[:, 0:192], O.mult)
         vtt("skb WU", "LCf", T.LCf[:], T.skb[:], T.WU[:, 12:24], O.add)
+        vts("PB", "sm0", T.sm[:, 0:128], T.PB[:, 0:128], 8.5, O.is_gt)
         vtt("mQ H LH", XW, T.X[:].indirect(T.LH[:]), T.mQ[:], T.H[:], O.add)
         vtc("LCf", "LC", T.LC[:], T.LCf[:])
+        if not last:
+            trail_a(0)
         vtc("xcut UL", XW, T.X[:].indirect(T.UL[:]), T.xcut[:])
         if last:
             for j in range(2):
                 fin(j)
-        vts("PC", "sm0", T.sm[:, 0:128], T.PC[:, 0:128], 8.5, O.is_gt)
         if not last:
             mm("onb skb", "PC", T.PC[:, 400:412], T.ONS[:], T.skb[:], True, True)
             act("PC", "jnk Sa", T.jnk[:], T.PC[:, 400:412], AF.Copy, accum_out=T.Sa[:])
         count(2)
         if not last:
-            trail_part(0, T.TR[:], "TR")
+            trail_b(0, T.TR[:], "TR")
+        vtt("sm0 CG", "cD0", T.cD[:, 0:128], T.sm[:, 0:128], T.CG[:, 0:128], O.mult)
+        if not last:
             trail_list(0)
             for c in range(2):
                 g2(c)
             mm("IDb " + Zn, "PZ", T.PZ[:, 0:192], T.IDb[:], T[Zn][:], True, True)
             diff(0, Zn)
-        vtt("sm0 CG", "cD0", T.cD[:, 0:128], T.sm[:, 0:128], T.CG[:, 0:128], O.mult)
-        vts("PB", "sm1", T.sm[:, 128:192], T.PB[:, 0:64], 8.5, O.is_gt)
+        vtt("cD0 TRf LC", "CN", T.CN[:].indirect(T.LC[:, 0:8]), T.cD[:, 0:128], T.TRf[:, 0:128], O.add)
+        vts("PC", "sm1", T.sm[:, 128:192], T.PC[:, 0:64], 8.5, O.is_gt)
         vtt("sm1 CG", "cD1", T.cD[:, 128:192], T.sm[:, 128:192], T.CG[:, 128:192], O.mult)
-        vtt("cD0 cD1 TRf LC", "CN", T.CN[:].indirect(T.LC[:]), T.cD[:], T.TRf[:], O.add)
+        vtt("cD1 TRf LC", "CN", T.CN[:].indirect(T.LC[:, 8:12]), T.cD[:, 128:192], T.TRf[:, 128:192], O.add)
         if not last:
             diff(1, Zn)
     for j in range(2):
         q = "sa"[j]
         outs.append((q, dma(q, "CN", "yl%d" % j, T.yl[:, 768 * j:768 * j + 768], T.CN[:, 768 * j:768 * j + 768])))
     for j in range(2):
-        trail_part(j, T.TF[:], "TF")
+        trail_a(j)
+        trail_b(j, T.TF[:], "TF")
     vts("TF0 TF1 REV", "go", T.sg[:], T.TF[:].indirect(T.REV[:]), float(CMID), O.add)
     outs.append(("s", dma("s", "go", "yg", T.yg[:], T.sg[:])))
     for q, s in outs:

from concourse.mybir import dt, AluOpType, AxisListType, ActivationFunctionType

W, U, B, T_STEPS = 3072, 1536, 192, 7
NB = B // 16
STARTS = [sum(B - 16 * m for m in range(i)) for i in range(NB + 1)]
RUN = STARTS[NB]
CMID = 1536
XB = 192
ROWS = [(t + 13) % 16 for t in range(T_STEPS)]

f32, b16, f16, i32, u16 = "float32", "bfloat16", "float16", "int32", "uint16"
_S = {
    "X": ([128, W + B], b16), "CN": ([128, 3840], f32), "TR": ([128, B], f16), "TRu": ([128, B], u16),
    "xraw": ([128, W], b16), "craw": ([128, U], i32), "traw": ([128, B], i32), "zraw": ([128, B], b16), "vraw": ([128, B], i32),
    "Ku": ([128, B], u16), "Kf": ([128, B], f32), "Kp": ([128, 6, 32], f16), "V": ([128, 6, 32], f16),
    "Xg1": ([128, W], b16), "Xg2": ([128, W], b16), "M1": ([128, NB, 256], b16),
    "A2": ([128, 3, 1024], b16), "IND": ([128, 3, 1024], b16), "AR": ([128, B], b16), "IR": ([128, B], b16),
    "Sc": ([128, B], f32), "ci": ([128, NB], i32), "cm": ([128, NB], i32), "ch": ([128, NB], i32), "cf": ([128, NB], f32),
    "CL": ([128, NB], u16), "VH": ([128, NB], u16), "UL": ([128, NB], u16), "ULf": ([128, 16], f32), "Dg": ([128, B], f16),
    "ACh": ([128, B], f16), "E": ([128, RUN], b16), "EC": ([128, RUN], b16), "sg": ([128, B], f32), "xcut": ([128, B], b16),
    "WD": ([128, B], f32), "WS": ([128, B], f32), "wu": ([128, 24], i32), "LU": ([128, NB], u16), "wb": ([128, NB], f32),
    "SQ": ([128, RUN], b16), "SW": ([128, RUN], b16), "NF": ([128, 32], f32), "e1": ([128, 24], f32), "WU": ([128, 24], f32),
    "LH": ([128, NB], u16), "LCf": ([128, NB], f32), "LC": ([128, NB], u16), "skb": ([128, NB], b16), "skr": ([128, B], b16),
    "H": ([128, B], b16), "Q": ([128, B], b16), "mQ": ([128, B], b16),
    "sm": ([128, B], f32), "tD": ([128, B], f32), "TRf": ([128, B], f32),
    "Co": ([128, B], f32), "CG": ([128, B], f32), "cD": ([128, B], f32), "TF": ([128, B], f32),
    "jnk": ([128, NB], f32), "Sa": ([128, 1], f32), "Si": ([128, 1], i32), "Sj": ([128, 1], i32),
    "LIM": ([128, 1], f32), "LB": ([128, 1], f32), "CB": ([128, 1], f32),
    "qi": ([128, 1], i32), "qa": ([128, 1], i32), "qm": ([128, 1], f32),
    "half": ([128, 2], f32), "io1": ([128, 48], f32), "io2": ([128, 48], f32), "io3": ([128, 48], f32),
    "REV": ([128, NB], u16), "RP": ([128, NB], u16), "ENDS": ([128, 2], u16), "DUM": ([128, 32], f32),
    "J16": ([128, B], f32), "DM": ([128, B], f32), "RST": ([128, B], f32), "A0": ([128, B], f32), "MK": ([128, RUN], b16), "MB": ([128, RUN], b16),
    "on": ([128, 144], f32), "on2": ([128, 144], f32), "BOf": ([128, 128], f32), "IDf": ([128, 128], f32), "sh0": ([128, 128], f32), "sh1": ([128, 128], f32),
    "BOh": ([128, 128], f16), "BOb": ([128, 128], b16), "PD1": ([128, 144], b16), "PDN": ([128, 144], b16), "PDH": ([128, 144], f16),
    "IDb": ([128, 128], b16), "NIb": ([128, 128], b16), "IDh": ([128, 128], f16), "IDm": ([128, T_STEPS * 128], f16), "RSL": ([128, T_STEPS * 128], f16),
    "SWP": ([128, 512], f16), "zero": ([128, B], b16), "ONS": ([128, 128], b16), "vsh": ([128, B], i32), "vfh": ([128, B], f16), "vrf": ([128, B], f32),
}
for _t in range(T_STEPS):
    _S["Z%d" % _t] = ([128, B], b16)
    if _t < T_STEPS - 1:
        _S["ZN%d" % _t] = ([128, B], b16)
SCRATCH = {k: ("sbuf", s, d) for k, (s, d) in _S.items()}
SCRATCH.update({
    "PA": ("psum", [128, 1024], f32), "PB": ("psum", [128, 1024], f32),
    "PZ": ("psum", [128, 512], f32), "PK": ("psum", [128, 512], f32), "PW": ("psum", [128, 512], f32), "PC": ("psum", [128, 512], f32),
})
SEMAPHORES = ["sv", "sp", "sa", "sg", "zsent"] + ["zs%d" % t for t in range(1, T_STEPS)] + ["d%d" % i for i in range(40)]


def rank_program(g, core, T, topo):
    rank = T.rank_of(core)
    if rank is None:
        return
    O, AF = AluOpType, ActivationFunctionType
    N = len(T.cores)
    ENG = {"v": g.vector, "p": g.tensor, "a": g.scalar, "g": g, "s": g.sync}
    cnt, known, wr, rd = {}, {}, {}, {}

    def need(q, src, n):
        if known.get((q, src), 0) < n:
            known[(q, src)] = n
            ENG[q].wait_ge(T.sem[src], n)

    def deps(q, R, Wr, par):
        own = "s" + q
        for k in R:
            if k in wr and not (q == "p" and wr[k][0] == own):
                need(q, wr[k][0], wr[k][1])
            if k[0] == "P":
                for s, n in rd.get(k, {}).items():
                    if s != own:
                        need(q, s, n)
        for k in Wr:
            if k in wr and not (wr[k][0] == own and (par or q == "p")):
                need(q, wr[k][0], wr[k][1])
            for s, n in rd.get(k, {}).items():
                if not (s == own and (par or q == "p")):
                    need(q, s, n)

    def note(src, n, R, Wr):
        for k in R:
            rd.setdefault(k, {})[src] = n
        for k in Wr:
            wr[k] = (src, n)
            rd[k] = {}

    def op(q, name, R, Wr, *a, par=False, **kw):
        R, Wr = R.split(), Wr.split()
        deps(q, R, Wr, par)
        if q == "v":
            e = g.vector
            fn = {"tc": e.tensor_copy, "ts": e.tensor_scalar, "tt": e.tensor_tensor, "scan": e.tensor_tensor_scan,
                  "ms": e.memset, "tr": e.transpose}[name]
        elif q == "a":
            fn = g.scalar.activation
        elif q == "p":
            fn = g.tensor.matmul
        else:
            fn = {"iota": g.iota, "sel": g.affine_select}[name]
        src = "s" + q
        cnt[src] = cnt.get(src, 0) + 1
        fn(*a, **kw).then_inc(T.sem[src], 1)
        note(src, cnt[src], R, Wr)

    nd = [0]

    def dma(q, R, Wr, out, in_):
        R, Wr = R.split(), Wr.split()
        deps(q, R, Wr, True)
        s = "d%d" % nd[0]
        nd[0] += 1
        ENG[q].dma_start(out, in_).then_inc(T.sem[s], 16)
        note(s, 16, R, Wr)
        return s

    def vtc(R, Wr, o, i, **k):
        op("v", "tc", R, Wr, o, i, **k)

    def vts(R, Wr, o, i, s1, o0, s2=None, o1=None, **k):
        if o1 is None:
            op("v", "ts", R, Wr, o, i, s1, None, o0, **k)
        else:
            op("v", "ts", R, Wr, o, i, s1, s2, o0, o1, **k)

    def vtt(R, Wr, o, a, b, f, **k):
        op("v", "tt", R, Wr, o, a, b, f, **k)

    def act(R, Wr, o, i, f=AF.Copy, **k):
        op("a", "act", R, Wr, o, i, f, **k)

    def mm(R, Wr, o, l, r, st, sp):
        op("p", "mm", R, Wr, o, l, r, st, sp)

    dma("s", "", "craw0", T.craw[:, 0:768], T.canal[:, 0:768])
    dma("a", "", "craw1", T.craw[:, 768:1536], T.canal[:, 768:1536])
    op("v", "ms", "", "vraw", T.vraw[:], 0)
    for j in range(8):
        dma("sa"[j % 2], "vraw" if j < 2 else "", "vr%d" % j, T.vraw[16 * j:16 * j + 1, :], T.cut[j:j + 1, :])
    VR = " ".join("vr%d" % j for j in range(8))
    dma("s", "", "traw", T.traw[:], T.trail[:])
    dma("a", "", "zraw", T.zraw[:], T.z[:])
    for j in range(4):
        dma("sa"[j % 2], "", "xraw%d" % j, T.xraw[:, 768 * j:768 * j + 768], T.x[:, 768 * j:768 * j + 768])
    op("g", "iota", "", "qi", T.qi[:], [[1, 1]], 0, 1)
    op("g", "iota", "", "J16", T.J16[:], [[0, 12], [1, 16]], 0, 0, allow_small_or_imprecise_dtypes=True)
    op("g", "iota", "", "io1", T.io1[:], [[16, 48]], 0, 0, allow_small_or_imprecise_dtypes=True)
    op("v", "ms", "", "on", T.on[:], 1.0)
    op("v", "ms", "", "on2", T.on2[:], 0.0)
    op("v", "ms", "on2", "on2", T.on2[:, 15::16], 1.0)
    op("v", "ms", "", "fon", T.sh0[:], 1.0)
    op("g", "sel", "on", "on", T.on[:, 0:128], T.on[:, 0:128], [[-16, 8], [0, 16]], O.is_ge, 0.0, 0, 1)
    op("g", "sel", "on", "BOf", T.BOf[:], T.on[:, 0:128], [[16, 8], [0, 16]], O.is_ge, 0.0, 15, -1)
    op("g", "sel", "on2", "on2", T.on2[:], T.on2[:], [[-16, 9], [0, 16]], O.is_ge, 0.0, 0, 1)
    op("g", "sel", "on2", "on2", T.on2[:], T.on2[:], [[16, 9], [0, 16]], O.is_ge, 0.0, 15, -1)
    op("g", "sel", "fon", "sh1", T.sh1[:], T.sh0[:], [[-1, 128]], O.is_equal, 0.0, -16, 1)
    op("g", "sel", "fon sh1", "sh0", T.sh0[:], T.sh0[:], [[-1, 128]], O.is_equal, 0.0, 16, 1)
    vts("qi", "qa", T.qa[:], T.qi[:], 15, O.bitwise_and)
    vtc("qa", "qm", T.qm[:], T.qa[:])
    vts("J16 qm", "DM", T.DM[:], T.J16[:], T.qm[:], O.is_equal)
    vts("io1 qm", "io2", T.io2[:, 0:12], T.io1[:, 0:12], T.qm[:], O.add)
    vts("io2", "REV", T.REV[:], T.io2[:, 0:12], -1.0, O.mult, 191.0, O.add)
    vts("J16", "A0", T.A0[:], T.J16[:], 0.0, O.not_equal)
    vtc("BOf", "BOh", T.BOh[:], T.BOf[:])
    vts("io1", "RP", T.RP[:], T.io1[:, 0:12], 0.0625, O.mult)
    vts("J16 qm", "IDf0", T.IDf[:], T.J16[:, 0:128], T.qm[:], O.is_equal)
    vtt("IDf0 BOf", "IDf", T.IDf[:], T.IDf[:], T.BOf[:], O.mult)
    act("IDf", "IDb", T.IDb[:], T.IDf[:])
    act("IDf", "NIb", T.NIb[:], T.IDf[:], AF.Copy, scale=-1.0)
    act("on2", "PDN", T.PDN[:], T.on2[:], AF.Copy, scale=-4096.0)
    act("BOf", "BOb", T.BOb[:], T.BOf[:])
    act("zraw REV", "Z0", T.Z0[:], T.zraw[:].indirect(T.REV[:]), AF.Copy, bias=float(XB))
    vtc("IDf", "IDh", T.IDh[:], T.IDf[:])
    for m in range(T_STEPS):
        op("g", "sel", "BOh", "RSL%d" % m, T.RSL[:, 128 * m:128 * m + 128], T.BOh[:], [[-16, 8], [0, 16]], O.is_equal, 0.0, -ROWS[m], 1)
        op("g", "sel", "IDh", "IDm%d" % m, T.IDm[:, 128 * m:128 * m + 128], T.IDh[:], [[0, 8], [1, 16]], O.not_equal, 0.0, -m, 0)
    vts("vraw " + VR, "vsh", T.vsh[:], T.vraw[:], 1, O.arith_shift_right)
    vtc("vsh", "vfh", T.vfh[:], T.vsh[:])
    mm("BOh vfh", "PW", T.PW[:, 0:192], T.BOh[:], T.vfh[:], True, True)
    act("PW", "vrf", T.vrf[:], T.PW[:, 0:192])
    vtc("craw0", "CN", T.CN[:, 0:768], T.craw[:, 0:768])
    vtt("vrf REV DM", "WD", T.WD[:], T.vrf[:].indirect(T.REV[:]), T.DM[:], O.mult)
    op("v", "scan", "A0 WD", "WS", T.WS[:], T.A0[:], T.WD[:], 0.0, O.mult, O.add)
    vtc("WS", "VH", T.VH[:], T.WS[:, 15::16])
    vtc("craw1", "CN", T.CN[:, 768:1536], T.craw[:, 768:1536], par=True)
    for j in range(3):
        act("xraw%d" % j, "X", T.X[:, 768 * j:768 * j + 768], T.xraw[:, 768 * j:768 * j + 768], AF.Copy, bias=float(XB), par=True)
    vts("xraw3", "X2", T.X[:, 2304:3072], T.xraw[:, 2304:3072], float(XB), O.add)
    act("on2", "PD1", T.PD1[:], T.on2[:])
    SWPS = "SWP00 SWP01 SWP10 SWP11"

    def trail_list(j):
        lo, hi = ((0, 128), (128, 192))[j]
        vts("TR%d" % j, "TRu%d" % j, T.TRu[:, lo:hi], T.TR[:, lo:hi], float(CMID), O.add)

    def consts_a():
        vts("traw REV", "TR0 TR1", T.TR[:], T.traw[:].indirect(T.REV[:]), -float(CMID), O.add)
        trail_list(0)
        trail_list(1)
        op("v", "ms", "", "zero", T.zero[:], 0.0)

    def consts_b():
        vts("qi", "Si", T.Si[:], T.qi[:], 16, O.bitwise_and)
        vts("Si", "half", T.half[:, 1:2], T.Si[:], 0.0625, O.mult)
        vts("half", "half0", T.half[:, 0:1], T.half[:, 1:2], -1.0, O.mult, 1.0, O.add)
        vts("IDf half half0", "SWP00", T.SWP[:, 0:128], T.IDf[:], T.half[:, 0:1], O.mult, -1.0, O.mult)
        vts("sh0 half half0", "SWP10", T.SWP[:, 256:384], T.sh0[:], T.half[:, 0:1], O.mult, -1.0, O.mult)
        vts("sh1 half half0", "SWP01", T.SWP[:, 128:256], T.sh1[:], T.half[:, 1:2], O.mult, -1.0, O.mult)
        vts("IDf half half0", "SWP11", T.SWP[:, 384:512], T.IDf[:], T.half[:, 1:2], O.mult, -1.0, O.mult)

    def consts_c():
        vts("J16", "RST0", T.RST[:], T.J16[:], 0.0, O.is_equal, 2.0e8, O.mult)
        vts("RST0", "RST", T.RST[:], T.RST[:], -1.0e8, O.add)
        op("v", "ms", "", "DUM", T.DUM[:], 0.0)
        vts("io2", "DUM", T.DUM[:, 0:12], T.io2[:, 0:12], float(W), O.add)
        vts("io2", "DUM", T.DUM[:, 12:24], T.io2[:, 0:12], float(U), O.add)
        vtc("io2", "io3", T.io3[:, 0:2], T.io2[:, 0:2])
        for lim in (12.0, 24.0):
            vts("io2", "io1b", T.io1[:, 16:18], T.io2[:, 0:2], lim, O.is_ge, -12.0, O.mult)
            vtt("io3 io1b", "io3", T.io3[:, 0:2], T.io3[:, 0:2], T.io1[:, 16:18], O.add)
        vts("io3", "io1b", T.io1[:, 16:18], T.io3[:, 0:2], -8.0, O.mult, 192.0, O.add)
        vts("io3", "io1c", T.io1[:, 32:34], T.io3[:, 0:2], 1.0, O.add)
        vtt("io1b io1c", "io3", T.io3[:, 4:6], T.io1[:, 16:18], T.io1[:, 32:34], O.mult)
        vts("io3", "ENDS", T.ENDS[:], T.io3[:, 4:6], -1.0, O.add)
        vtc("on2", "PDH", T.PDH[:], T.on2[:])
        op("v", "ms", "", "LIM", T.LIM[:], 18.5)
        op("v", "ms", "", "CB", T.CB[:], -1700.0)

    def consts_d():
        op("v", "ms", "", "onb", T.ONS[:], 1.0 / 2048.0)
        op("v", "ms", "", "MK", T.MK[:], 1.0)
        for ii in range(NB):
            vts("J16 qm MK", "MKs", T.MK[:, STARTS[ii]:STARTS[ii] + 16], T.J16[:, 0:16], T.qm[:], O.is_gt, par=True)
        vts("MKs MK", "MB", T.MB[:], T.MK[:], -1.0e8, O.mult, 1.0e8, O.add)

    XW = "X X2"
    Xw = T.X[:, 0:W]
    CNw = T.CN[:, 0:U]
    CH = [(0, 64), (64, 128), (128, 192)]
    XG2 = "Xg2.0 Xg2.1 Xg2.2"
    D2 = [("PA", T.PA), ("PB", T.PB), ("PA", T.PA)]
    CNT = [("PB", T.PB, 0), ("PB", T.PB, 64), ("PC", T.PC, 0)]

    def replay_rows(t):
        mm("RSL%d TR0 TR1" % t, "PW", T.PW[:, 0:192], T.RSL[:, 128 * t:128 * t + 128], T.TR[:], True, True)
        mm("IDh TR0 TR1", "PC", T.PC[:, 192:384], T.IDh[:], T.TR[:], True, True)
        act("PC", "TRf", T.TRf[:], T.PC[:, 192:384], AF.Copy, bias=float(CMID))

    def trail_a(j):
        lo, hi = ((0, 128), (128, 192))[j]
        vtt("sm%d PW" % j, "tD%d" % j, T.tD[:, lo:hi], T.sm[:, lo:hi], T.PW[:, 256 + lo:256 + hi], O.mult)

    def trail_b(j, out, nm):
        lo, hi = ((0, 128), (128, 192))[j]
        vtt("tD%d PK" % j, nm + "%d" % j, out[:, lo:hi], T.PK[:, 192 + lo:192 + hi], T.tD[:, lo:hi], O.subtract)

    def g2(c):
        act(XW + " TRu%d" % (c // 2), "Xg2.%d" % c, T.Xg2[:, 1024 * c:1024 * c + 1024], Xw.indirect(T.TRu[:, 64 * c:64 * c + 64]))

    def diff(c, Zk, k0=0, k1=16):
        nm, P = D2[c]
        for k in range(k0, k1):
            mm("IDb " + Zk, nm, P[:, 64 * k:64 * k + 64], T.IDb[:], T[Zk][:, 64 * c:64 * c + 64], True, False)
            mm("NIb Xg2.%d" % c, nm, P[:, 64 * k:64 * k + 64], T.NIb[:], T.Xg2[:, 1024 * c + k:1024 * c + 1024:16], False, True)

    def absd(c):
        nm, P = D2[c]
        act(nm, "A2.%d" % c, T.A2[:, c, :], P[:], AF.Abs)

    def thr(c):
        vts("A2.%d LIM" % c, "IND.%d" % c, T.IND[:, c, :], T.A2[:, c, :], T.LIM[:], O.is_gt)

    def count(c):
        nm, P, o = CNT[c]
        for k in range(16):
            mm("PD1 IND.%d" % c, nm, P[:, o:o + 64], T.PD1[:, 15 - k:143 - k], T.IND[:, c, 64 * k:64 * k + 64], k == 0, k == 15)

    def ttmax(c, fill=()):
        lo, hi = CH[c]
        for k in range(16):
            vtt("Xg1.%d PZ" % c, "M1.%d" % c, T.M1[:, 4 * c:4 * c + 4, k::16], T.Xg1[:, 1024 * c + k:1024 * c + 1024:16],
                T.PZ[:, lo:hi], O.max, par=True)
            if k % 4 == 3 and k // 4 < len(fill):
                fill[k // 4]()

    def score(c):
        lo, hi = CH[c]
        for p in range(16):
            mm("PDN M1.%d" % c, "PK", T.PK[:, lo:hi], T.PDN[:, 15 - p:143 - p], T.M1[:, 4 * c:4 * c + 4, 16 * p:16 * p + 16],
               False, c == 2 and p == 15)

    outs = []

    def fin(j):
        c0 = 1536 * j
        if j:
            act(XW, "xo1", T.xraw[:, c0:c0 + 1536], T.X[:, c0:c0 + 1536], AF.Copy, bias=-float(XB))
        else:
            vts(XW, "xo0", T.xraw[:, c0:c0 + 1536], T.X[:, c0:c0 + 1536], -float(XB), O.add)
        q = "sa"[j]
        outs.append((q, dma(q, "xo%d" % j, "yx%d" % j, T.yx[:, c0:c0 + 1536], T.xraw[:, c0:c0 + 1536])))

    for t in range(T_STEPS):
        r = ROWS[t]
        last = t == T_STEPS - 1
        Zk, Zn = "Z%d" % t, "Z%d" % (t + 1)
        Z = T[Zk]
        vtc("CN VH", "Ku", T.Ku[:], CNw.indirect(T.VH[:]))
        act("CN VH", "Kf", T.Kf[:], CNw.indirect(T.VH[:]), AF.Copy, bias=-float(CMID))
        for c in (1, 2):
            act(XW + " Ku", "Xg1.%d" % c, T.Xg1[:, 1024 * c:1024 * c + 1024], Xw.indirect(T.Ku[:, 64 * c:64 * c + 64]))
        vtc(XW + " Ku", "Xg1.0", T.Xg1[:, 0:1024], Xw.indirect(T.Ku[:, 0:64]))
        if not t:
            consts_a()
            mm("IDb " + Zk, "PZ", T.PZ[:, 0:192], T.IDb[:], Z[:], True, True)
        else:
            vtc("Sa", "Si", T.Si[:], T.Sa[:])
            trail_a(1)
            vts("Si", "Sj", T.Sj[:], T.Si[:], 3, O.bitwise_and)
            trail_b(1, T.TR[:], "TR")
            vts("Sj", "LIM", T.LIM[:], T.Sj[:], 18.5, O.add)
            trail_list(1)
        replay_rows(t)
        mm("BOb zero", "PK", T.PK[:, 0:192], T.BOb[:], T.zero[:], True, False)
        ttmax(0)
        score(0)
        if not t:
            consts_b()
            for c in range(2):
                g2(c)
                diff(c, Zk)
        absd(0)
        g2(2)
        absd(1)
        fills = [
            lambda: [vts("Kf", "Kp", T.Kp[:, :, 16 * q:16 * q + 16], T.Kf[:, 96 * q:96 * q + 96], -1.0, O.mult, par=True) for q in range(2)],
            lambda: op("v", "tr", "Kp", "V", T.V[:], T.Kp[:]),
            lambda: vtt("PW DM", "WD", T.WD[:], T.PW[:, 0:192], T.DM[:], O.mult),
            lambda: op("v", "scan", "A0 WD", "WS", T.WS[:], T.A0[:], T.WD[:], 0.0, O.mult, O.add),
            lambda: vts("WS", "wi", T.wu[:, 0:12], T.WS[:, 15::16], float(CMID), O.add),
            lambda: vts("wi", "ui", T.wu[:, 12:24], T.wu[:, 0:12], 1, O.arith_shift_right),
            lambda: vtc("ui", "LU", T.LU[:], T.wu[:, 12:24]),
            lambda: vts("ui", "wb", T.wb[:], T.wu[:, 12:24], -2.0, O.mult, float(CMID) - 0.5, O.add)]
        ttmax(1, fills[:4])
        for q in range(2):
            for h in range(2):
                mm("V " + SWPS, "PK", T.PK[:, 96 * q:96 * q + 96], T.SWP[:, 256 * h + 128 * q:256 * h + 128 * q + 128],
                   T.V[:, :, 16 * h:16 * h + 16], False, False)
        score(1)
        ttmax(2, fills[4:])
        score(2)
        diff(2, Zk, 0, 8)
        if not t:
            consts_c()
        thr(0)
        count(0)
        op("v", "scan", "RST PK", "Sc", T.Sc[:], T.RST[:], T.PK[:, 0:192], 0.0, O.max, O.min)
        act("CN LU", "Co", T.Co[:], CNw.indirect(T.LU[:]), AF.Copy, bias=-float(CMID))
        vts("Sc", "ci", T.ci[:], T.Sc[:, 15::16], float(CMID), O.add)
        vts("ci", "cm", T.cm[:], T.ci[:], 4095, O.bitwise_and)
        vts("cm", "cf", T.cf[:], T.cm[:], -float(CMID), O.add)
        vtc("cm", "CL", T.CL[:], T.cm[:])
        if not last:
            vts("cm", "ch", T.ch[:], T.cm[:], 1, O.arith_shift_right)
        vtt("cf RP DM", "Dg", T.Dg[:], T.cf[:].indirect(T.RP[:]), T.DM[:], O.mult)
        if not last:
            vtt(XW + " CL " + Zk, "sg", T.sg[:], Xw.indirect(T.CL[:]), Z[:], O.add)
        mm("BOh Dg", "PZ", T.PZ[:, 192:384], T.BOh[:], T.Dg[:], True, True)
        mm("IDm%d TR0 TR1" % t, "PK", T.PK[:, 192:384], T.IDm[:, 128 * t:128 * t + 128], T.TR[:], True, False)
        mm("PDH Dg", "PK", T.PK[:, 192:384], T.PDH[:, 15 - t:143 - t], T.Dg[:], False, True)
        if not last:
            vtc("ch", "VH", T.VH[:], T.ch[:])
            vts("sg", "ZN%d" % t, T["ZN%d" % t][:], T.sg[:], 0.5, O.mult, -0.25, O.add)
            dst = T.cores[(rank + 1 + t % (N - 1)) % N]
            rid, pid, _e = topo.addr(dst)
            need("g", wr["ZN%d" % t][0], wr["ZN%d" % t][1])
            g.remote_dma(T[Zn][:], T["ZN%d" % t][:], T.sem["zs%d" % (t + 1)], T.sem.zsent, pid, rid, topo.mask(core, dst))
            src = T.cores[(rank - 1 - t % (N - 1)) % N]
            note("zs%d" % (t + 1), len(topo.engines(src, core)), [], [Zn])
        vtt("Co PC", "CG", T.CG[:], T.Co[:], T.PC[:, 192:384], O.subtract)
        mm("IDb " + Zk, "PK", T.PK[:, 0:192], T.IDb[:], Z[:], True, False)
        mm("NIb " + XG2, "PK", T.PK[:, 0:192], T.NIb[:], T.Xg2[:, r::16], False, True)
        act("PK", "AR", T.AR[:], T.PK[:, 0:192], AF.Abs)
        if not t:
            consts_d()
        vtc("PZ", "ACh", T.ACh[:], T.PZ[:, 192:384])
        for ii in range(NB):
            vts("ACh cf", "E", T.E[:, STARTS[ii]:STARTS[ii + 1]], T.ACh[:, 16 * ii:192], T.cf[:, ii:ii + 1], O.is_equal, par=True)
        mm("IDb " + XG2, "PZ", T.PZ[:, 192:384], T.IDb[:], T.Xg2[:, r::16], True, False)
        mm("IDb " + Zk, "PZ", T.PZ[:, 192:384], T.IDb[:], Z[:], False, True)
        diff(2, Zk, 8, 16)
        act("PZ", "H", T.H[:], T.PZ[:, 192:384], AF.Copy, scale=0.5, bias=-0.25)
        for ii in range(NB):
            act("PW wb", "SQ", T.SQ[:, STARTS[ii]:STARTS[ii + 1]], T.PW[:, 16 * ii:192], AF.Square, bias=T.wb[:, ii:ii + 1], par=True)
        vts("AR LIM", "IR", T.IR[:], T.AR[:], T.LIM[:], O.is_gt)
        vts(XG2, "Q", T.Q[:], T.Xg2[:, r::16], 4.0, O.add, XB + 63.0, O.min)
        mm("BOb IR", "PC", T.PC[:, 192:384], T.BOb[:], T.IR[:], True, True)
        for p in range(16):
            mm("PD1 IR", "PC", T.PC[:, 384:396], T.PD1[:, 15 - p:143 - p], T.IR[:, p::16], p == 0, p == 15)
        mm("IDb Q", "PZ", T.PZ[:, 0:192], T.IDb[:], T.Q[:], True, False)
        mm("NIb H", "PZ", T.PZ[:, 0:192], T.NIb[:], T.H[:], False, True)
        act(XW + " CL", "xcut", T.xcut[:], Xw.indirect(T.CL[:]), AF.Copy, scale=0.5, bias=XB / 2 - 0.25)
        act("PC CB", "skr", T.skr[:], T.PC[:, 192:384], AF.Sigmoid, bias=T.CB[:], scale=200.0)
        absd(2)
        act("LIM", "LB", T.LB[:], T.LIM[:], AF.Copy, scale=-200.0)
        act("A2.2 LB", "IND.2", T.IND[:, 2, :], T.A2[:, 2, :], AF.Sigmoid, bias=T.LB[:], scale=200.0)
        op("v", "scan", "E MK MKs", "EC", T.EC[:], T.E[:], T.MK[:], 0.0, O.max, O.mult)
        thr(1)
        count(1)
        for q in range(2):
            mm("IDm%d Kp" % t, "PW", T.PW[:, 256 + 96 * q:352 + 96 * q], T.IDm[:, 128 * t:128 * t + 128], T.Kp[:, :, 16 * q:16 * q + 16], True, False)
            mm("IDm%d TR0 TR1" % t, "PW", T.PW[:, 256 + 96 * q:352 + 96 * q], T.IDm[:, 128 * t:128 * t + 128], T.TR[:, 96 * q:96 * q + 96], False, True)
        op("v", "scan", "SQ MB", "SW", T.SW[:], T.SQ[:], T.MB[:], 1.0e8, O.min, O.max)
        vtt("EC ENDS DUM", "ULf", T.ULf[:], T.EC[:].indirect(T.ENDS[:, 0:1]), T.DUM[:, 0:16], O.mult)
        vts("SW ENDS", "NF", T.NF[:], T.SW[:].indirect(T.ENDS[:]), 1.0, O.is_lt)
        vtt("ULf cm", "ULg", T.ULf[:, 0:12], T.ULf[:, 0:12], T.cm[:], O.max)
        vtt("NF DUM", "e1", T.e1[:], T.NF[:, 0:24], T.DUM[:, 0:24], O.mult)
        vtc("ULg", "UL", T.UL[:], T.ULf[:, 0:12])
        vtt("e1 wi ui", "WU", T.WU[:], T.e1[:], T.wu[:], O.max)
        vts("PC", "skb", T.skb[:], T.PC[:, 384:396], 8.5, O.is_gt, 2048.0, O.mult)
        vtc("WU", "LH", T.LH[:], T.WU[:, 0:12])
        vtt("skr PZ", "mQ", T.mQ[:], T.skr[:], T.PZ[:, 0:192], O.mult)
        vtt("skb WU", "LCf", T.LCf[:], T.skb[:], T.WU[:, 12:24], O.add)
        vts("PB", "sm0", T.sm[:, 0:128], T.PB[:, 0:128], 8.5, O.is_gt)
        vtt("mQ H LH", XW, T.X[:].indirect(T.LH[:]), T.mQ[:], T.H[:], O.add)
        vtc("LCf", "LC", T.LC[:], T.LCf[:])
        if not last:
            trail_a(0)
        vtc("xcut UL", XW, T.X[:].indirect(T.UL[:]), T.xcut[:])
        if last:
            for j in range(2):
                fin(j)
        if not last:
            mm("onb skb", "PC", T.PC[:, 400:412], T.ONS[:], T.skb[:], True, True)
            act("PC", "jnk Sa", T.jnk[:], T.PC[:, 400:412], AF.Copy, accum_out=T.Sa[:])
        count(2)
        if not last:
            trail_b(0, T.TR[:], "TR")
        vtt("sm0 CG", "cD0", T.cD[:, 0:128], T.sm[:, 0:128], T.CG[:, 0:128], O.mult)
        if not last:
            trail_list(0)
            for c in range(2):
                g2(c)
            mm("IDb " + Zn, "PZ", T.PZ[:, 0:192], T.IDb[:], T[Zn][:], True, True)
            diff(0, Zn)
        vtt("cD0 TRf LC", "CN", T.CN[:].indirect(T.LC[:, 0:8]), T.cD[:, 0:128], T.TRf[:, 0:128], O.add)
        vts("PC", "sm1", T.sm[:, 128:192], T.PC[:, 0:64], 8.5, O.is_gt)
        vtt("sm1 CG", "cD1", T.cD[:, 128:192], T.sm[:, 128:192], T.CG[:, 128:192], O.mult)
        vtt("cD1 TRf LC", "CN", T.CN[:].indirect(T.LC[:, 8:12]), T.cD[:, 128:192], T.TRf[:, 128:192], O.add)
        if not last:
            diff(1, Zn)
    for j in range(2):
        q = "sa"[j]
        outs.append((q, dma(q, "CN", "yl%d" % j, T.yl[:, 768 * j:768 * j + 768], T.CN[:, 768 * j:768 * j + 768])))
    for j in range(2):
        trail_a(j)
        trail_b(j, T.TF[:], "TF")
    vts("TF0 TF1 REV", "go", T.sg[:], T.TF[:].indirect(T.REV[:]), float(CMID), O.add)
    outs.append(("s", dma("s", "go", "yg", T.yg[:], T.sg[:])))
    for q, s in outs:
        need(q, s, 16)
    g.wait_ge(T.sem.zsent, sum(len(topo.engines(core, T.cores[(rank + 1 + t % (N - 1)) % N])) for t in range(T_STEPS - 1)))
